import numpy as np
import ml_dtypes


def mxq(x, axis, fmt="e4m3"):
    dtype, down = {"e4m3": (ml_dtypes.float8_e4m3fn, 7), "e5m2": (ml_dtypes.float8_e5m2, 14)}[fmt]
    v = np.moveaxis(np.asarray(x, np.float32).astype(ml_dtypes.bfloat16).astype(np.float64), axis, -1)
    blocks = v.reshape(v.shape[:-1] + (-1, 32))
    amax = np.abs(blocks).max(-1, keepdims=True)
    byte = np.maximum(np.where(amax > 0, np.frexp(amax)[1] - 1 + 127, 0) - down, 1)
    scale = np.exp2(byte - 127.0)
    codes = (blocks / scale).astype(np.float32).astype(dtype).astype(np.float64)
    return np.moveaxis((codes * scale).reshape(v.shape), -1, axis)


WIDE = False


def mx_kscale(k):
    if not WIDE:
        return np.ones(k)
    levels = np.array([18, -18])
    if k % 512:
        return np.exp2(np.random.permutation(np.resize(levels, k // 32))).repeat(32)
    a = np.empty((k // 512, 16))
    for p in range(k // 512):
        a[p, :8] = np.random.permutation(np.resize(levels, 8))
        for g in range(8):
            far = levels[np.abs(levels - a[p, g]) >= 10]
            a[p, g + 8] = far[np.random.randint(len(far))]
    return np.exp2(a.ravel()).repeat(32)


def f64(x):
    return np.asarray(x).astype(np.float64)


def striped(idx):
    return np.tile(np.asarray(idx).reshape(-1, 16).T, (8, 1)).astype(np.uint16)


def unstriped(offs):
    return offs[:16].T.reshape(-1).astype(np.int64)


B, N, T, D, R, TU = 1, 512, 2048, 512, 512, 2048


def setup_inputs():
    n = np.random.standard_normal
    idx = np.random.permutation(T)[:B * N]
    uidx = np.random.permutation(TU)[:B * R]
    s = mx_kscale(D)[:, None]
    z = np.ones(TU)
    z[uidx] = mx_kscale(B * R)
    u = np.ones(T)
    u[idx] = mx_kscale(B * N)
    r = np.random.uniform(0.5, 2.0, T) * u
    ur = np.random.uniform(0.5, 2.0, TU) * z
    return {
        "uT": (n((D, TU)) * s / ur).astype(np.float32),
        "vT": (n((D, T)) * (1.00 / np.sqrt(D)) / s / r).astype(np.float32),
        "y": (2 * np.random.randint(0, 2, (B, R, N)) - 1).astype(np.float32),
        "us": ur[uidx].reshape(B, R, 1).astype(np.float32),
        "ts": np.tile(r, (128, 1)).astype(np.float32),
        "offs": striped(idx),
        "uoffs": striped(uidx),
    }


def reference(uT, vT, y, us, ts, offs, uoffs):
    idx = unstriped(offs)
    pick = lambda x: x[:, idx].reshape(x.shape[0], B, N).transpose(1, 0, 2)
    uidx = unstriped(uoffs)
    w = pick(f64(vT))
    x = f64(uT)[:, uidx].reshape(D, B, R).transpose(1, 0, 2)
    a = mxq(x, 1, "e4m3").transpose(0, 2, 1) @ mxq(w, 1, "e4m3")
    sc = f64(us) * pick(f64(ts))[:, :1, :]
    a = a * sc
    g = -f64(y) / (1.0 + np.exp(f64(y) * a))
    h = sc * g
    dv = mxq(x, 2, "e4m3") @ mxq(h, 1, "e5m2")
    gv = np.zeros((D, T))
    gv[:, idx] = dv.transpose(1, 0, 2).reshape(D, B * N)
    du = mxq(w, 2, "e4m3") @ mxq(h, 2, "e5m2").transpose(0, 2, 1)
    gu = np.zeros((D, TU))
    gu[:, uidx] = du.transpose(1, 0, 2).reshape(D, B * R)
    return gv, gu

@@ -1,0 +1,211 @@
+from contextlib import ExitStack
+
+import concourse.mybir as mybir
+from concourse.masks import make_identity
+
+P = 128
+PACK = 4
+D = 512
+LISTED = 512
+TABLE = 2048
+CHUNK = 128
+WINDOWS = 2
+
+FLOPS = 3 * 2 * D * LISTED * LISTED
+BYTES = 4 * (4 * D * TABLE + LISTED * LISTED + LISTED + TABLE) + 2 * 2 * P * (LISTED // 16)
+
+F32 = mybir.dt.float32
+BF16 = mybir.dt.bfloat16
+U32 = mybir.dt.uint32
+U16 = mybir.dt.uint16
+U8 = mybir.dt.uint8
+E4M3 = mybir.dt.float8_e4m3fn_x4
+E5M2 = mybir.dt.float8_e5m2_x4
+MULT = mybir.AluOpType.mult
+SIGMOID = mybir.ActivationFunctionType.Sigmoid
+
+
+def tile_attend_gmf_sig_vu_kernel(tc, uT, vT, y, us, ts, offs, uoffs, out_0, out_1):
+    nc = tc.nc
+    with ExitStack() as ctx:
+        keep = ctx.enter_context(tc.tile_pool(name="keep", bufs=1))
+        work = ctx.enter_context(tc.tile_pool(name="work", bufs=3))
+        turn_psum = ctx.enter_context(tc.psum_pool(name="turn_psum", bufs=2))
+        score_psum = ctx.enter_context(tc.psum_pool(name="score_psum", bufs=4))
+        grad_psum = ctx.enter_context(tc.psum_pool(name="grad_psum", bufs=2))
+
+        def mx_operand(name):
+            codes = keep.tile([P, LISTED], U32, name=name + "_codes", align_bytes=64)
+            scales = keep.tile([P, LISTED], U8, name=name + "_scales", align_bytes=64)
+            return codes, scales
+
+        def quantize(operand, fmt, source, cols):
+            codes, scales = operand
+            nc.vector.quantize_mx(
+                out=codes[:, cols].bitcast(fmt),
+                scales=scales[:, cols],
+                in_=source[:, cols, :].rearrange("p c t -> p (c t)"),
+            )
+
+        def matmul(out, lhs, lhs_cols, rhs, rhs_fmt, rhs_cols):
+            nc.tensor.matmul_mx(
+                out=out,
+                lhsT=lhs[0][:, lhs_cols].bitcast(E4M3),
+                lhsT_scale=lhs[1][:, lhs_cols],
+                rhs=rhs[0][:, rhs_cols].bitcast(rhs_fmt),
+                rhs_scale=rhs[1][:, rhs_cols],
+                start=True,
+                stop=True,
+            )
+
+        def block(k):
+            return slice(k * P, (k + 1) * P)
+
+        u_list = keep.tile([P, LISTED // 16], U16, name="u_list")
+        v_list = keep.tile([P, LISTED // 16], U16, name="v_list")
+        u_planes = [keep.tile([P, TABLE], F32, name="u_plane%d" % t) for t in range(PACK)]
+        v_planes = [keep.tile([P, TABLE], F32, name="v_plane%d" % t) for t in range(PACK)]
+        labels = keep.tile([P, PACK, LISTED], F32, name="labels")
+        row_scale = keep.tile([P, PACK], F32, name="row_scale")
+        ts_window = keep.tile([P, TABLE], F32, name="ts_window")
+        u_rows = uT.rearrange("(p t) c -> t p c", t=PACK)
+        v_rows = vT.rearrange("(p t) c -> t p c", t=PACK)
+
+        nc.sync.dma_start(u_planes[0][:], u_rows[0])
+        nc.sync.dma_start(u_list[:], uoffs)
+        nc.sync.dma_start(v_list[:], offs)
+        for t in range(1, PACK):
+            nc.sync.dma_start(u_planes[t][:], u_rows[t])
+        nc.sync.dma_start(labels[:], y.rearrange("b (p t) i -> p (b t) i", t=PACK))
+        for t in range(PACK):
+            nc.sync.dma_start(v_planes[t][:], v_rows[t])
+
+        nc.vector.memset(ts_window[:], 0.0)
+        nc.scalar.dma_start(ts_window[0:1, :], ts[0:1, :])
+        nc.scalar.dma_start(row_scale[:], us.rearrange("b (p t) o -> p (b t o)", t=PACK))
+
+        ident_f32 = keep.tile([P, P], F32, name="ident_f32")
+        ident_bf16 = keep.tile([P, P], BF16, name="ident_bf16")
+        make_identity(nc, ident_f32[:])
+        make_identity(nc, ident_bf16[:])
+        warm = keep.tile([P, 1], F32, name="warm")
+        nc.scalar.activation(warm[:], ident_f32[:, 0:1], SIGMOID)
+
+        v_windows = [keep.tile([P, TABLE], F32, name="v_window%d" % k) for k in range(WINDOWS)]
+        u_windows = [keep.tile([P, TABLE], F32, name="u_window%d" % k) for k in range(WINDOWS)]
+        for window in v_windows + u_windows:
+            nc.gpsimd.memset(window[:], 0.0)
+
+        ts_listed = keep.tile([P, LISTED], F32, name="ts_listed")
+        nc.vector.tensor_copy(ts_listed[:], ts_window[:].indirect(v_list[:]))
+        ts_turned = turn_psum.tile([P, PACK, P], F32, name="ts_turned", tag="turn")
+        for k in range(PACK):
+            nc.tensor.transpose(ts_turned[:, k, :], ts_listed[:, block(k)], ident_f32[:])
+        neg_ts = keep.tile([P, PACK], F32, name="neg_ts")
+        nc.vector.tensor_scalar(neg_ts[:], ts_turned[:, :, 0], -1.0, None, MULT)
+        neg_ts_rows = grad_psum.tile([P, LISTED], F32, name="neg_ts_rows", tag="grad")
+        for k in range(PACK):
+            nc.tensor.transpose(neg_ts_rows[:, block(k)], neg_ts[:, k : k + 1].to_broadcast([P, P]), ident_f32[:])
+
+        x_planes = keep.tile([P, PACK, LISTED], F32, name="x_planes")
+        x_by_r = keep.tile([P, D, PACK], BF16, name="x_by_r", align_bytes=64)
+        xq_r = mx_operand("xq_r")
+        for t in range(PACK):
+            nc.vector.tensor_copy(x_planes[:, t, :], u_planes[t][:].indirect(u_list[:]))
+            turned = turn_psum.tile([P, PACK, P], F32, name="x_turned", tag="turn")
+            for j in range(PACK):
+                nc.tensor.transpose(turned[:, j, :], x_planes[:, t, j:LISTED:PACK], ident_f32[:])
+            nc.scalar.copy(x_by_r[:, block(t), :], turned[:].rearrange("m j p -> m p j"))
+        x_by_d = keep.tile([P, LISTED, PACK], BF16, name="x_by_d", align_bytes=64)
+        nc.scalar.copy(
+            x_by_d[:].rearrange("p (j m) t -> p m j t", j=PACK),
+            x_planes[:].rearrange("p t (m j) -> p m j t", j=PACK),
+        )
+        xq_d = mx_operand("xq_d")
+        quantize(xq_d, E4M3, x_by_d, slice(0, LISTED))
+        quantize(xq_r, E4M3, x_by_r, slice(0, D))
+
+        q_planes = keep.tile([P, PACK, LISTED], F32, name="q_planes")
+        for t in range(PACK):
+            nc.vector.scalar_tensor_tensor(
+                q_planes[:, t, :], labels[:, t, :], row_scale[:, t : t + 1], neg_ts_rows[:], MULT, MULT
+            )
+        q = keep.tile([P, LISTED, PACK], F32, name="q")
+        nc.scalar.copy(q[:], q_planes[:].rearrange("p t i -> p i t"))
+
+        w_by_d = keep.tile([P, LISTED, PACK], BF16, name="w_by_d", align_bytes=64)
+        w_by_i = keep.tile([P, D, PACK], BF16, name="w_by_i", align_bytes=64)
+        wq_d = mx_operand("wq_d")
+        wq_i = mx_operand("wq_i")
+
+        def turn(dst, src, t):
+            turned = turn_psum.tile([P, PACK, P], BF16, name="turned", tag="turn")
+            for j in range(PACK):
+                nc.tensor.transpose(turned[:, j, :], src[:, j:LISTED:PACK, t], ident_bf16[:])
+            nc.scalar.copy(dst[:, block(t), :], turned[:].rearrange("m j p -> m p j"))
+
+        last = PACK - 1
+        for t in range(last):
+            nc.vector.tensor_copy(w_by_d[:, :, t], v_planes[t][:].indirect(v_list[:]))
+            turn(w_by_i, w_by_d, t)
+            quantize(wq_i, E4M3, w_by_i, block(t))
+        half = LISTED // 2
+        for n in range(2):
+            cols = slice(n * half, (n + 1) * half)
+            nc.vector.tensor_copy(
+                w_by_d[:, cols, last], v_planes[last][:].indirect(v_list[:, n * half // 16 : (n + 1) * half // 16])
+            )
+        for n in range(2):
+            quantize(wq_d, E4M3, w_by_d, slice(n * half, (n + 1) * half))
+
+        h = keep.tile([P, LISTED, PACK], BF16, name="h", align_bytes=64)
+        hq_r = mx_operand("hq_r")
+        for c in range(LISTED // CHUNK):
+            cols = slice(c * CHUNK, (c + 1) * CHUNK)
+            score = score_psum.tile([P, PACK, CHUNK], F32, name="score")
+            for t in range(PACK):
+                matmul(score[:, t, :], xq_d, block(t), wq_d, E4M3, cols)
+            logit = work.tile([P, CHUNK, PACK], F32, name="logit")
+            nc.vector.tensor_tensor(logit[:], score[:].rearrange("p t i -> p i t"), q[:, cols, :], MULT)
+            prob = work.tile([P, CHUNK, PACK], F32, name="prob")
+            nc.scalar.activation(prob[:], logit[:], SIGMOID)
+            nc.vector.tensor_tensor(h[:, cols, :], prob[:], q[:, cols, :], MULT)
+            quantize(hq_r, E5M2, h, cols)
+
+        h_by_i = keep.tile([P, LISTED, PACK], BF16, name="h_by_i", align_bytes=64)
+        hq_i = mx_operand("hq_i")
+        dv_rows = out_0.rearrange("(p t) c -> t p c", t=PACK)
+        du_rows = out_1.rearrange("(p t) c -> t p c", t=PACK)
+        everything = slice(0, LISTED)
+
+        def caption_grad(t):
+            grad = grad_psum.tile([P, LISTED], F32, name="dv", tag="grad")
+            matmul(grad[:], xq_r, block(t), hq_r, E5M2, everything)
+            dense = work.tile([P, LISTED], F32, name="dense")
+            nc.scalar.copy(dense[:], grad[:])
+            window = v_windows[t % WINDOWS]
+            nc.vector.tensor_copy(window[:].indirect(v_list[:]), dense[:])
+            nc.sync.dma_start(dv_rows[t], window[:])
+
+        def image_grad(t):
+            grad = grad_psum.tile([P, PACK, P], F32, name="du", tag="grad")
+            matmul(grad[:].rearrange("p j m -> p (j m)"), wq_i, block(t), hq_i, E5M2, everything)
+            dense = work.tile([P, P, PACK], F32, name="dense")
+            nc.scalar.copy(dense[:], grad[:].rearrange("p j m -> p m j"))
+            window = u_windows[t % WINDOWS]
+            nc.vector.tensor_copy(window[:].indirect(u_list[:]), dense[:].rearrange("p m j -> p (m j)"))
+            nc.sync.dma_start(du_rows[t], window[:])
+
+        caption_grad(0)
+        caption_grad(1)
+        for t in range(PACK):
+            turn(h_by_i, h, t)
+        quantize(hq_i, E5M2, h_by_i, everything)
+        turn(w_by_i, w_by_d, last)
+        quantize(wq_i, E4M3, w_by_i, block(last))
+        image_grad(0)
+        caption_grad(2)
+        image_grad(1)
+        caption_grad(3)
+        image_grad(2)
+        image_grad(3)

@@ -34,9 +34,9 @@ def tile_attend_gmf_sig_vu_kernel(tc, uT, vT, y, us, ts, offs, uoffs, out_0, out
         score_psum = ctx.enter_context(tc.psum_pool(name="score_psum", bufs=4))
         grad_psum = ctx.enter_context(tc.psum_pool(name="grad_psum", bufs=2))
 
-        def mx_operand(name):
-            codes = keep.tile([P, LISTED], U32, name=name + "_codes", align_bytes=64)
-            scales = keep.tile([P, LISTED], U8, name=name + "_scales", align_bytes=64)
+        def mx_operand(name, width=LISTED, tag=""):
+            codes = keep.tile([P, width], U32, name=name + "_codes", tag=tag, align_bytes=64)
+            scales = keep.tile([P, width], U8, name=name + "_scales", align_bytes=64)
             return codes, scales
 
         def quantize(operand, fmt, source, cols):
@@ -63,26 +63,22 @@ def tile_attend_gmf_sig_vu_kernel(tc, uT, vT, y, us, ts, offs, uoffs, out_0, out
 
         u_list = keep.tile([P, LISTED // 16], U16, name="u_list")
         v_list = keep.tile([P, LISTED // 16], U16, name="v_list")
-        u_planes = [keep.tile([P, TABLE], F32, name="u_plane%d" % t) for t in range(PACK)]
-        v_planes = [keep.tile([P, TABLE], F32, name="v_plane%d" % t) for t in range(PACK)]
+        u_planes = [keep.tile([P, TABLE], F32, name="u_plane", tag="plane%d" % t, align_bytes=64) for t in range(PACK)]
         labels = keep.tile([P, PACK, LISTED], F32, name="labels")
         row_scale = keep.tile([P, PACK], F32, name="row_scale")
         ts_window = keep.tile([P, TABLE], F32, name="ts_window")
         u_rows = uT.rearrange("(p t) c -> t p c", t=PACK)
         v_rows = vT.rearrange("(p t) c -> t p c", t=PACK)
 
-        nc.sync.dma_start(u_planes[0][:], u_rows[0])
-        nc.sync.dma_start(u_list[:], uoffs)
+        nc.scalar.dma_start(ts_window[P - 1 : P, :], ts[0:1, :])
+        nc.scalar.dma_start(row_scale[:], us.rearrange("b (p t) o -> p (b t o)", t=PACK))
         nc.sync.dma_start(v_list[:], offs)
-        for t in range(1, PACK):
-            nc.sync.dma_start(u_planes[t][:], u_rows[t])
+        nc.sync.dma_start(u_list[:], uoffs)
         nc.sync.dma_start(labels[:], y.rearrange("b (p t) i -> p (b t) i", t=PACK))
         for t in range(PACK):
-            nc.sync.dma_start(v_planes[t][:], v_rows[t])
+            nc.sync.dma_start(u_planes[t][:], u_rows[t])
 
-        nc.vector.memset(ts_window[:], 0.0)
-        nc.scalar.dma_start(ts_window[0:1, :], ts[0:1, :])
-        nc.scalar.dma_start(row_scale[:], us.rearrange("b (p t) o -> p (b t o)", t=PACK))
+        nc.vector.memset(ts_window[0 : P - 1, :], 0.0)
 
         ident_f32 = keep.tile([P, P], F32, name="ident_f32")
         ident_bf16 = keep.tile([P, P], BF16, name="ident_bf16")
@@ -102,28 +98,10 @@ def tile_attend_gmf_sig_vu_kernel(tc, uT, vT, y, us, ts, offs, uoffs, out_0, out
         for k in range(PACK):
             nc.tensor.transpose(ts_turned[:, k, :], ts_listed[:, block(k)], ident_f32[:])
         neg_ts = keep.tile([P, PACK], F32, name="neg_ts")
-        nc.vector.tensor_scalar(neg_ts[:], ts_turned[:, :, 0], -1.0, None, MULT)
+        nc.vector.tensor_scalar(neg_ts[:], ts_turned[:, :, P - 1], -1.0, None, MULT)
         neg_ts_rows = grad_psum.tile([P, LISTED], F32, name="neg_ts_rows", tag="grad")
         for k in range(PACK):
             nc.tensor.transpose(neg_ts_rows[:, block(k)], neg_ts[:, k : k + 1].to_broadcast([P, P]), ident_f32[:])
-
-        x_planes = keep.tile([P, PACK, LISTED], F32, name="x_planes")
-        x_by_r = keep.tile([P, D, PACK], BF16, name="x_by_r", align_bytes=64)
-        xq_r = mx_operand("xq_r")
-        for t in range(PACK):
-            nc.vector.tensor_copy(x_planes[:, t, :], u_planes[t][:].indirect(u_list[:]))
-            turned = turn_psum.tile([P, PACK, P], F32, name="x_turned", tag="turn")
-            for j in range(PACK):
-                nc.tensor.transpose(turned[:, j, :], x_planes[:, t, j:LISTED:PACK], ident_f32[:])
-            nc.scalar.copy(x_by_r[:, block(t), :], turned[:].rearrange("m j p -> m p j"))
-        x_by_d = keep.tile([P, LISTED, PACK], BF16, name="x_by_d", align_bytes=64)
-        nc.scalar.copy(
-            x_by_d[:].rearrange("p (j m) t -> p m j t", j=PACK),
-            x_planes[:].rearrange("p t (m j) -> p m j t", j=PACK),
-        )
-        xq_d = mx_operand("xq_d")
-        quantize(xq_d, E4M3, x_by_d, slice(0, LISTED))
-        quantize(xq_r, E4M3, x_by_r, slice(0, D))
 
         q_planes = keep.tile([P, PACK, LISTED], F32, name="q_planes")
         for t in range(PACK):
@@ -133,36 +111,66 @@ def tile_attend_gmf_sig_vu_kernel(tc, uT, vT, y, us, ts, offs, uoffs, out_0, out
         q = keep.tile([P, LISTED, PACK], F32, name="q")
         nc.scalar.copy(q[:], q_planes[:].rearrange("p t i -> p i t"))
 
+        x_planes = keep.tile([P, PACK, LISTED], F32, name="x_planes")
+        x_by_r = keep.tile([P, D, PACK], BF16, name="x_by_r", align_bytes=64)
+        last = PACK - 1
+
+        def turn_images(t):
+            turned = turn_psum.tile([P, PACK, P], F32, name="x_turned", tag="turn")
+            for j in range(PACK):
+                nc.tensor.transpose(turned[:, j, :], x_planes[:, t, j:LISTED:PACK], ident_f32[:])
+            nc.scalar.copy(x_by_r[:, block(t), :], turned[:].rearrange("m j p -> m p j"))
+
+        for t in range(PACK):
+            nc.vector.tensor_copy(x_planes[:, t, :], u_planes[t][:].indirect(u_list[:]))
+            if t < last:
+                turn_images(t)
+        x_by_d = keep.tile([P, LISTED, PACK], BF16, name="x_by_d", align_bytes=64)
+        nc.scalar.copy(
+            x_by_d[:].rearrange("p (j m) t -> p m j t", j=PACK),
+            x_planes[:].rearrange("p t (m j) -> p m j t", j=PACK),
+        )
+        turn_images(last)
+        v_planes = [keep.tile([P, TABLE], F32, name="v_plane", tag="plane%d" % t, align_bytes=64) for t in range(PACK)]
+        for t in range(PACK):
+            nc.sync.dma_start(v_planes[t][:], v_rows[t])
+
         w_by_d = keep.tile([P, LISTED, PACK], BF16, name="w_by_d", align_bytes=64)
         w_by_i = keep.tile([P, D, PACK], BF16, name="w_by_i", align_bytes=64)
         wq_d = mx_operand("wq_d")
         wq_i = mx_operand("wq_i")
 
-        def turn(dst, src, t):
-            turned = turn_psum.tile([P, PACK, P], BF16, name="turned", tag="turn")
+        def turn(dst, src, t, pool=turn_psum, tag="turn"):
+            turned = pool.tile([P, PACK, P], BF16, name="turned", tag=tag)
             for j in range(PACK):
                 nc.tensor.transpose(turned[:, j, :], src[:, j:LISTED:PACK, t], ident_bf16[:])
             nc.scalar.copy(dst[:, block(t), :], turned[:].rearrange("m j p -> m p j"))
 
-        last = PACK - 1
         for t in range(last):
             nc.vector.tensor_copy(w_by_d[:, :, t], v_planes[t][:].indirect(v_list[:]))
             turn(w_by_i, w_by_d, t)
-            quantize(wq_i, E4M3, w_by_i, block(t))
+            if t == 0:
+                xq_d = mx_operand("xq_d", tag="plane0")
+                quantize(xq_d, E4M3, x_by_d, slice(0, LISTED))
         half = LISTED // 2
         for n in range(2):
             cols = slice(n * half, (n + 1) * half)
             nc.vector.tensor_copy(
                 w_by_d[:, cols, last], v_planes[last][:].indirect(v_list[:, n * half // 16 : (n + 1) * half // 16])
             )
-        for n in range(2):
-            quantize(wq_d, E4M3, w_by_d, slice(n * half, (n + 1) * half))
+        for cols in (block(0), block(1), slice(half, LISTED)):
+            quantize(wq_d, E4M3, w_by_d, cols)
+        xq_r = mx_operand("xq_r", tag="plane%d" % last)
+        quantize(xq_r, E4M3, x_by_r, slice(0, D))
 
         h = keep.tile([P, LISTED, PACK], BF16, name="h", align_bytes=64)
-        hq_r = mx_operand("hq_r")
+        padded = mx_operand("hq_r", half + LISTED)
+        for part in padded:
+            nc.gpsimd.memset(part[:, 0:half], 0)
+        hq_r = [part[:, half:] for part in padded]
         for c in range(LISTED // CHUNK):
             cols = slice(c * CHUNK, (c + 1) * CHUNK)
-            score = score_psum.tile([P, PACK, CHUNK], F32, name="score")
+            score = score_psum.tile([P, PACK, CHUNK], F32, name="score", tag="score")
             for t in range(PACK):
                 matmul(score[:, t, :], xq_d, block(t), wq_d, E4M3, cols)
             logit = work.tile([P, CHUNK, PACK], F32, name="logit")
@@ -178,13 +186,20 @@ def tile_attend_gmf_sig_vu_kernel(tc, uT, vT, y, us, ts, offs, uoffs, out_0, out
         du_rows = out_1.rearrange("(p t) c -> t p c", t=PACK)
         everything = slice(0, LISTED)
 
-        def caption_grad(t):
+        def early_caption_grad(t):
+            grad = grad_psum.tile([P, LISTED], F32, name="dv", tag="grad")
+            matmul(grad[:], xq_r, block(t), padded, E5M2, everything)
+            dense = work.tile([P, half], F32, name="dense")
+            nc.scalar.copy(dense[:], grad[:, half:])
+            nc.vector.tensor_copy(v_windows[t][:].indirect(v_list[:, 0 : half // 16]), dense[:])
+
+        def caption_grad(t, first):
             grad = grad_psum.tile([P, LISTED], F32, name="dv", tag="grad")
             matmul(grad[:], xq_r, block(t), hq_r, E5M2, everything)
-            dense = work.tile([P, LISTED], F32, name="dense")
-            nc.scalar.copy(dense[:], grad[:])
+            dense = work.tile([P, LISTED - first], F32, name="dense")
+            nc.scalar.copy(dense[:], grad[:, first:])
             window = v_windows[t % WINDOWS]
-            nc.vector.tensor_copy(window[:].indirect(v_list[:]), dense[:])
+            nc.vector.tensor_copy(window[:].indirect(v_list[:, first // 16 :]), dense[:])
             nc.sync.dma_start(dv_rows[t], window[:])
 
         def image_grad(t):
@@ -196,16 +211,18 @@ def tile_attend_gmf_sig_vu_kernel(tc, uT, vT, y, us, ts, offs, uoffs, out_0, out
             nc.vector.tensor_copy(window[:].indirect(u_list[:]), dense[:].rearrange("p m j -> p (m j)"))
             nc.sync.dma_start(du_rows[t], window[:])
 
-        caption_grad(0)
-        caption_grad(1)
+        early_caption_grad(0)
+        early_caption_grad(1)
+        caption_grad(0, half)
+        caption_grad(1, half)
         for t in range(PACK):
             turn(h_by_i, h, t)
         quantize(hq_i, E5M2, h_by_i, everything)
-        turn(w_by_i, w_by_d, last)
-        quantize(wq_i, E4M3, w_by_i, block(last))
+        turn(w_by_i, w_by_d, last, score_psum, "score")
+        quantize(wq_i, E4M3, w_by_i, everything)
         image_grad(0)
-        caption_grad(2)
+        caption_grad(2, 0)
         image_grad(1)
-        caption_grad(3)
+        caption_grad(3, 0)
         image_grad(2)
         image_grad(3)

@@ -9,7 +9,8 @@ D = 512
 LISTED = 512
 TABLE = 2048
 CHUNK = 128
-WINDOWS = 2
+V_WINDOWS = 3
+U_WINDOWS = 2
 
 FLOPS = 3 * 2 * D * LISTED * LISTED
 BYTES = 4 * (4 * D * TABLE + LISTED * LISTED + LISTED + TABLE) + 2 * 2 * P * (LISTED // 16)
@@ -87,8 +88,8 @@ def tile_attend_gmf_sig_vu_kernel(tc, uT, vT, y, us, ts, offs, uoffs, out_0, out
         warm = keep.tile([P, 1], F32, name="warm")
         nc.scalar.activation(warm[:], ident_f32[:, 0:1], SIGMOID)
 
-        v_windows = [keep.tile([P, TABLE], F32, name="v_window%d" % k) for k in range(WINDOWS)]
-        u_windows = [keep.tile([P, TABLE], F32, name="u_window%d" % k) for k in range(WINDOWS)]
+        v_windows = [keep.tile([P, TABLE], F32, name="v_window%d" % k) for k in range(V_WINDOWS)]
+        u_windows = [keep.tile([P, TABLE], F32, name="u_window%d" % k) for k in range(U_WINDOWS)]
         for window in v_windows + u_windows:
             nc.gpsimd.memset(window[:], 0.0)
 
@@ -138,7 +139,6 @@ def tile_attend_gmf_sig_vu_kernel(tc, uT, vT, y, us, ts, offs, uoffs, out_0, out
         w_by_d = keep.tile([P, LISTED, PACK], BF16, name="w_by_d", align_bytes=64)
         w_by_i = keep.tile([P, D, PACK], BF16, name="w_by_i", align_bytes=64)
         wq_d = mx_operand("wq_d")
-        wq_i = mx_operand("wq_i")
 
         def turn(dst, src, t, pool=turn_psum, tag="turn"):
             turned = pool.tile([P, PACK, P], BF16, name="turned", tag=tag)
@@ -149,10 +149,12 @@ def tile_attend_gmf_sig_vu_kernel(tc, uT, vT, y, us, ts, offs, uoffs, out_0, out
         for t in range(last):
             nc.vector.tensor_copy(w_by_d[:, :, t], v_planes[t][:].indirect(v_list[:]))
             turn(w_by_i, w_by_d, t)
-            if t == 0:
-                xq_d = mx_operand("xq_d", tag="plane0")
+            if t == 1:
+                xq_d = mx_operand("xq_d", tag="plane1")
                 quantize(xq_d, E4M3, x_by_d, slice(0, LISTED))
         half = LISTED // 2
+        wq_i = mx_operand("wq_i", tag="plane2")
+        quantize(wq_i, E4M3, w_by_i, slice(0, half))
         for n in range(2):
             cols = slice(n * half, (n + 1) * half)
             nc.vector.tensor_copy(
@@ -194,11 +196,11 @@ def tile_attend_gmf_sig_vu_kernel(tc, uT, vT, y, us, ts, offs, uoffs, out_0, out
             nc.vector.tensor_copy(v_windows[t][:].indirect(v_list[:, 0 : half // 16]), dense[:])
 
         def caption_grad(t, first):
-            grad = grad_psum.tile([P, LISTED], F32, name="dv", tag="grad")
+            grad = turn_psum.tile([P, LISTED], F32, name="dv", tag="turn")
             matmul(grad[:], xq_r, block(t), hq_r, E5M2, everything)
             dense = work.tile([P, LISTED - first], F32, name="dense")
             nc.scalar.copy(dense[:], grad[:, first:])
-            window = v_windows[t % WINDOWS]
+            window = v_windows[t % V_WINDOWS]
             nc.vector.tensor_copy(window[:].indirect(v_list[:, first // 16 :]), dense[:])
             nc.sync.dma_start(dv_rows[t], window[:])
 
@@ -207,22 +209,21 @@ def tile_attend_gmf_sig_vu_kernel(tc, uT, vT, y, us, ts, offs, uoffs, out_0, out
             matmul(grad[:].rearrange("p j m -> p (j m)"), wq_i, block(t), hq_i, E5M2, everything)
             dense = work.tile([P, P, PACK], F32, name="dense")
             nc.scalar.copy(dense[:], grad[:].rearrange("p j m -> p m j"))
-            window = u_windows[t % WINDOWS]
+            window = u_windows[t % U_WINDOWS]
             nc.vector.tensor_copy(window[:].indirect(u_list[:]), dense[:].rearrange("p m j -> p (m j)"))
             nc.sync.dma_start(du_rows[t], window[:])
 
-        early_caption_grad(0)
-        early_caption_grad(1)
-        caption_grad(0, half)
-        caption_grad(1, half)
+        for t in range(V_WINDOWS):
+            early_caption_grad(t)
+        turn(w_by_i, w_by_d, last, score_psum, "score")
+        quantize(wq_i, E4M3, w_by_i, slice(half, D))
         for t in range(PACK):
             turn(h_by_i, h, t)
         quantize(hq_i, E5M2, h_by_i, everything)
-        turn(w_by_i, w_by_d, last, score_psum, "score")
-        quantize(wq_i, E4M3, w_by_i, everything)
+        for t in range(V_WINDOWS):
+            caption_grad(t, half)
         image_grad(0)
-        caption_grad(2, 0)
         image_grad(1)
-        caption_grad(3, 0)
+        caption_grad(last, 0)
         image_grad(2)
         image_grad(3)

@@ -85,8 +85,6 @@ def tile_attend_gmf_sig_vu_kernel(tc, uT, vT, y, us, ts, offs, uoffs, out_0, out
         ident_bf16 = keep.tile([P, P], BF16, name="ident_bf16")
         make_identity(nc, ident_f32[:])
         make_identity(nc, ident_bf16[:])
-        warm = keep.tile([P, 1], F32, name="warm")
-        nc.scalar.activation(warm[:], ident_f32[:, 0:1], SIGMOID)
 
         v_windows = [keep.tile([P, TABLE], F32, name="v_window%d" % k) for k in range(V_WINDOWS)]
         u_windows = [keep.tile([P, TABLE], F32, name="u_window%d" % k) for k in range(U_WINDOWS)]

@@ -9,8 +9,9 @@ D = 512
 LISTED = 512
 TABLE = 2048
 CHUNK = 128
-V_WINDOWS = 3
-U_WINDOWS = 2
+V_WINDOWS = 4
+U_WINDOWS = 3
+EARLY = 3
 
 FLOPS = 3 * 2 * D * LISTED * LISTED
 BYTES = 4 * (4 * D * TABLE + LISTED * LISTED + LISTED + TABLE) + 2 * 2 * P * (LISTED // 16)
@@ -31,6 +32,7 @@ def tile_attend_gmf_sig_vu_kernel(tc, uT, vT, y, us, ts, offs, uoffs, out_0, out
     with ExitStack() as ctx:
         keep = ctx.enter_context(tc.tile_pool(name="keep", bufs=1))
         work = ctx.enter_context(tc.tile_pool(name="work", bufs=3))
+        staged = ctx.enter_context(tc.tile_pool(name="staged", bufs=6))
         turn_psum = ctx.enter_context(tc.psum_pool(name="turn_psum", bufs=2))
         score_psum = ctx.enter_context(tc.psum_pool(name="score_psum", bufs=4))
         grad_psum = ctx.enter_context(tc.psum_pool(name="grad_psum", bufs=2))
@@ -189,39 +191,45 @@ def tile_attend_gmf_sig_vu_kernel(tc, uT, vT, y, us, ts, offs, uoffs, out_0, out
         def early_caption_grad(t):
             grad = grad_psum.tile([P, LISTED], F32, name="dv", tag="grad")
             matmul(grad[:], xq_r, block(t), padded, E5M2, everything)
-            dense = work.tile([P, half], F32, name="dense")
+            dense = staged.tile([P, half], F32, name="dense")
             nc.scalar.copy(dense[:], grad[:, half:])
             nc.vector.tensor_copy(v_windows[t][:].indirect(v_list[:, 0 : half // 16]), dense[:])
 
-        def caption_grad(t, first):
-            grad = turn_psum.tile([P, LISTED], F32, name="dv", tag="turn")
+        def caption_grad(t, first, pool, tag):
+            grad = pool.tile([P, LISTED], F32, name="dv", tag=tag)
             matmul(grad[:], xq_r, block(t), hq_r, E5M2, everything)
-            dense = work.tile([P, LISTED - first], F32, name="dense")
+            dense = staged.tile([P, LISTED - first], F32, name="dense")
             nc.scalar.copy(dense[:], grad[:, first:])
             window = v_windows[t % V_WINDOWS]
             nc.vector.tensor_copy(window[:].indirect(v_list[:, first // 16 :]), dense[:])
             nc.sync.dma_start(dv_rows[t], window[:])
 
         def image_grad(t):
-            grad = grad_psum.tile([P, PACK, P], F32, name="du", tag="grad")
-            matmul(grad[:].rearrange("p j m -> p (j m)"), wq_i, block(t), hq_i, E5M2, everything)
-            dense = work.tile([P, P, PACK], F32, name="dense")
-            nc.scalar.copy(dense[:], grad[:].rearrange("p j m -> p m j"))
+            grad = grad_psum.tile([P, LISTED], F32, name="du", tag="grad")
+            matmul(grad[:], wq_i, block(t), hq_i, E5M2, everything)
+            dense = staged.tile([P, LISTED], F32, name="dense")
+            nc.scalar.copy(dense[:], grad[:])
             window = u_windows[t % U_WINDOWS]
-            nc.vector.tensor_copy(window[:].indirect(u_list[:]), dense[:].rearrange("p m j -> p (m j)"))
+            nc.vector.tensor_copy(window[:].indirect(u_list[:]), dense[:])
             nc.sync.dma_start(du_rows[t], window[:])
 
-        for t in range(V_WINDOWS):
+        for t in range(EARLY):
             early_caption_grad(t)
         turn(w_by_i, w_by_d, last, score_psum, "score")
         quantize(wq_i, E4M3, w_by_i, slice(half, D))
-        for t in range(PACK):
-            turn(h_by_i, h, t)
+        for t in range(EARLY - 1):
+            caption_grad(t, half, grad_psum, "grad")
+        h_words = h[:].rearrange("p i t -> p (i t)").bitcast(F32)
+        for u in range(2):
+            turned = turn_psum.tile([P, PACK, P], F32, name="h_turned", tag="turn")
+            for j in range(PACK):
+                nc.tensor.transpose(turned[:, j, :], h_words[:, 2 * j + u : 2 * LISTED : 2 * PACK], ident_f32[:])
+            nc.scalar.copy(
+                h_by_i[:].rearrange("m (p u e) j -> m u p e j", u=2, e=2)[:, u],
+                turned[:].rearrange("m j p -> m (j p)").bitcast(BF16).rearrange("m (j p e) -> m p e j", j=PACK, e=2),
+            )
         quantize(hq_i, E5M2, h_by_i, everything)
-        for t in range(V_WINDOWS):
-            caption_grad(t, half)
-        image_grad(0)
-        image_grad(1)
-        caption_grad(last, 0)
-        image_grad(2)
-        image_grad(3)
+        caption_grad(EARLY - 1, half, turn_psum, "turn")
+        caption_grad(last, 0, turn_psum, "turn")
+        for t in range(PACK):
+            image_grad(t)

@@ -66,7 +66,7 @@ def tile_attend_gmf_sig_vu_kernel(tc, uT, vT, y, us, ts, offs, uoffs, out_0, out
 
         u_list = keep.tile([P, LISTED // 16], U16, name="u_list")
         v_list = keep.tile([P, LISTED // 16], U16, name="v_list")
-        u_planes = [keep.tile([P, TABLE], F32, name="u_plane", tag="plane%d" % t, align_bytes=64) for t in range(PACK)]
+        u_planes = [keep.tile([P, TABLE], F32, name="u_plane%d" % t) for t in range(PACK)]
         labels = keep.tile([P, PACK, LISTED], F32, name="labels")
         row_scale = keep.tile([P, PACK], F32, name="row_scale")
         ts_window = keep.tile([P, TABLE], F32, name="ts_window")
@@ -98,7 +98,7 @@ def tile_attend_gmf_sig_vu_kernel(tc, uT, vT, y, us, ts, offs, uoffs, out_0, out
         ts_turned = turn_psum.tile([P, PACK, P], F32, name="ts_turned", tag="turn")
         for k in range(PACK):
             nc.tensor.transpose(ts_turned[:, k, :], ts_listed[:, block(k)], ident_f32[:])
-        neg_ts = keep.tile([P, PACK], F32, name="neg_ts")
+        neg_ts = keep.tile([P, PACK], F32, name="neg_ts", tag="x_planes")
         nc.vector.tensor_scalar(neg_ts[:], ts_turned[:, :, P - 1], -1.0, None, MULT)
         neg_ts_rows = grad_psum.tile([P, LISTED], F32, name="neg_ts_rows", tag="grad")
         for k in range(PACK):
@@ -112,7 +112,7 @@ def tile_attend_gmf_sig_vu_kernel(tc, uT, vT, y, us, ts, offs, uoffs, out_0, out
         q = keep.tile([P, LISTED, PACK], F32, name="q")
         nc.scalar.copy(q[:], q_planes[:].rearrange("p t i -> p i t"))
 
-        x_planes = keep.tile([P, PACK, LISTED], F32, name="x_planes")
+        x_planes = keep.tile([P, PACK, LISTED], F32, name="x_planes", tag="x_planes")
         x_by_r = keep.tile([P, D, PACK], BF16, name="x_by_r", align_bytes=64)
         last = PACK - 1
 

@@ -75,9 +75,9 @@ def tile_attend_gmf_sig_vu_kernel(tc, uT, vT, y, us, ts, offs, uoffs, out_0, out
 
         nc.scalar.dma_start(ts_window[P - 1 : P, :], ts[0:1, :])
         nc.scalar.dma_start(row_scale[:], us.rearrange("b (p t) o -> p (b t o)", t=PACK))
+        nc.sync.dma_start(labels[:], y.rearrange("b (p t) i -> p (b t) i", t=PACK))
         nc.sync.dma_start(v_list[:], offs)
         nc.sync.dma_start(u_list[:], uoffs)
-        nc.sync.dma_start(labels[:], y.rearrange("b (p t) i -> p (b t) i", t=PACK))
         for t in range(PACK):
             nc.sync.dma_start(u_planes[t][:], u_rows[t])
 
@@ -211,7 +211,11 @@ def tile_attend_gmf_sig_vu_kernel(tc, uT, vT, y, us, ts, offs, uoffs, out_0, out
             nc.scalar.copy(dense[:], grad[:])
             window = u_windows[t % U_WINDOWS]
             nc.vector.tensor_copy(window[:].indirect(u_list[:]), dense[:])
-            nc.sync.dma_start(du_rows[t], window[:])
+            if t < last:
+                nc.sync.dma_start(du_rows[t], window[:])
+            else:
+                nc.sync.dma_start(du_rows[t][:, 0 : TABLE // 2], window[:, 0 : TABLE // 2])
+                nc.scalar.dma_start(du_rows[t][:, TABLE // 2 :], window[:, TABLE // 2 :])
 
         for t in range(EARLY):
             early_caption_grad(t)

@@ -84,9 +84,7 @@ def tile_attend_gmf_sig_vu_kernel(tc, uT, vT, y, us, ts, offs, uoffs, out_0, out
         nc.vector.memset(ts_window[0 : P - 1, :], 0.0)
 
         ident_f32 = keep.tile([P, P], F32, name="ident_f32")
-        ident_bf16 = keep.tile([P, P], BF16, name="ident_bf16")
         make_identity(nc, ident_f32[:])
-        make_identity(nc, ident_bf16[:])
 
         v_windows = [keep.tile([P, TABLE], F32, name="v_window%d" % k) for k in range(V_WINDOWS)]
         u_windows = [keep.tile([P, TABLE], F32, name="u_window%d" % k) for k in range(U_WINDOWS)]
@@ -137,24 +135,14 @@ def tile_attend_gmf_sig_vu_kernel(tc, uT, vT, y, us, ts, offs, uoffs, out_0, out
             nc.sync.dma_start(v_planes[t][:], v_rows[t])
 
         w_by_d = keep.tile([P, LISTED, PACK], BF16, name="w_by_d", align_bytes=64)
-        w_by_i = keep.tile([P, D, PACK], BF16, name="w_by_i", align_bytes=64)
         wq_d = mx_operand("wq_d")
-
-        def turn(dst, src, t, pool=turn_psum, tag="turn"):
-            turned = pool.tile([P, PACK, P], BF16, name="turned", tag=tag)
-            for j in range(PACK):
-                nc.tensor.transpose(turned[:, j, :], src[:, j:LISTED:PACK, t], ident_bf16[:])
-            nc.scalar.copy(dst[:, block(t), :], turned[:].rearrange("m j p -> m p j"))
 
         for t in range(last):
             nc.vector.tensor_copy(w_by_d[:, :, t], v_planes[t][:].indirect(v_list[:]))
-            turn(w_by_i, w_by_d, t)
             if t == 1:
                 xq_d = mx_operand("xq_d", tag="plane1")
                 quantize(xq_d, E4M3, x_by_d, slice(0, LISTED))
         half = LISTED // 2
-        wq_i = mx_operand("wq_i", tag="plane2")
-        quantize(wq_i, E4M3, w_by_i, slice(0, half))
         for n in range(2):
             cols = slice(n * half, (n + 1) * half)
             nc.vector.tensor_copy(
@@ -175,7 +163,10 @@ def tile_attend_gmf_sig_vu_kernel(tc, uT, vT, y, us, ts, offs, uoffs, out_0, out
             score = score_psum.tile([P, PACK, CHUNK], F32, name="score", tag="score")
             for t in range(PACK):
                 matmul(score[:, t, :], xq_d, block(t), wq_d, E4M3, cols)
-            logit = work.tile([P, CHUNK, PACK], F32, name="logit")
+            if c < LISTED // CHUNK - 1:
+                logit = work.tile([P, CHUNK, PACK], F32, name="logit")
+            else:
+                logit = keep.tile([P, CHUNK, PACK], F32, name="last_logit", tag="w_by_i", align_bytes=64)
             nc.vector.tensor_tensor(logit[:], score[:].rearrange("p t i -> p i t"), q[:, cols, :], MULT)
             prob = work.tile([P, CHUNK, PACK], F32, name="prob")
             nc.scalar.activation(prob[:], logit[:], SIGMOID)
@@ -219,8 +210,18 @@ def tile_attend_gmf_sig_vu_kernel(tc, uT, vT, y, us, ts, offs, uoffs, out_0, out
 
         for t in range(EARLY):
             early_caption_grad(t)
-        turn(w_by_i, w_by_d, last, score_psum, "score")
-        quantize(wq_i, E4M3, w_by_i, slice(half, D))
+        w_by_i = keep.tile([P, D, PACK], BF16, name="w_by_i", tag="w_by_i", align_bytes=64)
+        w_words = w_by_d[:].rearrange("p i t -> p (i t)").bitcast(F32)
+        for u in range(2):
+            turned = score_psum.tile([P, PACK, P], F32, name="w_turned", tag="score")
+            for j in range(PACK):
+                nc.tensor.transpose(turned[:, j, :], w_words[:, 2 * j + u : 2 * LISTED : 2 * PACK], ident_f32[:])
+            nc.scalar.copy(
+                w_by_i[:].rearrange("m (u e p) j -> m u e p j", u=2, e=2)[:, u],
+                turned[:].rearrange("m j p -> m (j p)").bitcast(BF16).rearrange("m (j p e) -> m e p j", j=PACK, e=2),
+            )
+        wq_i = mx_operand("wq_i")
+        quantize(wq_i, E4M3, w_by_i, everything)
         for t in range(EARLY - 1):
             caption_grad(t, half, grad_psum, "grad")
         h_words = h[:].rearrange("p i t -> p (i t)").bitcast(F32)

@@ -102,7 +102,7 @@ def tile_attend_gmf_sig_vu_kernel(tc, uT, vT, y, us, ts, offs, uoffs, out_0, out
         for k in range(PACK):
             nc.tensor.transpose(neg_ts_rows[:, block(k)], neg_ts[:, k : k + 1].to_broadcast([P, P]), ident_f32[:])
 
-        q_planes = keep.tile([P, PACK, LISTED], F32, name="q_planes")
+        q_planes = keep.tile([P, PACK, LISTED], F32, name="q_planes", tag="q_planes", align_bytes=64)
         for t in range(PACK):
             nc.vector.scalar_tensor_tensor(
                 q_planes[:, t, :], labels[:, t, :], row_scale[:, t : t + 1], neg_ts_rows[:], MULT, MULT
@@ -139,6 +139,9 @@ def tile_attend_gmf_sig_vu_kernel(tc, uT, vT, y, us, ts, offs, uoffs, out_0, out
 
         for t in range(last):
             nc.vector.tensor_copy(w_by_d[:, :, t], v_planes[t][:].indirect(v_list[:]))
+            if t == 0:
+                xq_r = mx_operand("xq_r", tag="plane0")
+                quantize(xq_r, E4M3, x_by_r, slice(0, D))
             if t == 1:
                 xq_d = mx_operand("xq_d", tag="plane1")
                 quantize(xq_d, E4M3, x_by_d, slice(0, LISTED))
@@ -150,28 +153,30 @@ def tile_attend_gmf_sig_vu_kernel(tc, uT, vT, y, us, ts, offs, uoffs, out_0, out
             )
         for cols in (block(0), block(1), slice(half, LISTED)):
             quantize(wq_d, E4M3, w_by_d, cols)
-        xq_r = mx_operand("xq_r", tag="plane%d" % last)
-        quantize(xq_r, E4M3, x_by_r, slice(0, D))
 
-        h = keep.tile([P, LISTED, PACK], BF16, name="h", align_bytes=64)
         padded = mx_operand("hq_r", half + LISTED)
         for part in padded:
             nc.gpsimd.memset(part[:, 0:half], 0)
         hq_r = [part[:, half:] for part in padded]
-        for c in range(LISTED // CHUNK):
-            cols = slice(c * CHUNK, (c + 1) * CHUNK)
+        chunks = LISTED // CHUNK
+        probs = []
+        for c in range(chunks):
             score = score_psum.tile([P, PACK, CHUNK], F32, name="score", tag="score")
             for t in range(PACK):
-                matmul(score[:, t, :], xq_d, block(t), wq_d, E4M3, cols)
-            if c < LISTED // CHUNK - 1:
-                logit = work.tile([P, CHUNK, PACK], F32, name="logit")
+                matmul(score[:, t, :], xq_d, block(t), wq_d, E4M3, block(c))
+            if c < chunks - 1:
+                logit = work.tile([P, PACK, CHUNK], F32, name="logit")
             else:
-                logit = keep.tile([P, CHUNK, PACK], F32, name="last_logit", tag="w_by_i", align_bytes=64)
-            nc.vector.tensor_tensor(logit[:], score[:].rearrange("p t i -> p i t"), q[:, cols, :], MULT)
-            prob = work.tile([P, CHUNK, PACK], F32, name="prob")
-            nc.scalar.activation(prob[:], logit[:], SIGMOID)
-            nc.vector.tensor_tensor(h[:, cols, :], prob[:], q[:, cols, :], MULT)
-            quantize(hq_r, E5M2, h, cols)
+                logit = keep.tile([P, PACK, CHUNK], F32, name="last_logit", tag="w_by_i", align_bytes=64)
+            nc.vector.tensor_tensor(logit[:], score[:], q_planes[:, :, block(c)], MULT)
+            prob = keep.tile([P, CHUNK, PACK], F32, name="prob%d" % c)
+            nc.scalar.activation(prob[:], logit[:].rearrange("p t i -> p i t"), SIGMOID)
+            probs.append(prob)
+        h = keep.tile([P, LISTED, PACK], BF16, name="h", tag="q_planes", align_bytes=64)
+        for c in range(chunks):
+            nc.vector.tensor_tensor(h[:, block(c), :], probs[c][:], q[:, block(c), :], MULT)
+            if c >= 2:
+                quantize(hq_r, E5M2, h, slice((c - 2) * half, (c - 1) * half))
 
         h_by_i = keep.tile([P, LISTED, PACK], BF16, name="h_by_i", align_bytes=64)
         hq_i = mx_operand("hq_i")

@@ -66,7 +66,9 @@ def tile_attend_gmf_sig_vu_kernel(tc, uT, vT, y, us, ts, offs, uoffs, out_0, out
 
         u_list = keep.tile([P, LISTED // 16], U16, name="u_list")
         v_list = keep.tile([P, LISTED // 16], U16, name="v_list")
-        u_planes = [keep.tile([P, TABLE], F32, name="u_plane%d" % t) for t in range(PACK)]
+        u_planes = [
+            keep.tile([P, TABLE], F32, name="u_plane%d" % t, tag="u_plane%d" % t, align_bytes=64) for t in range(PACK)
+        ]
         labels = keep.tile([P, PACK, LISTED], F32, name="labels")
         row_scale = keep.tile([P, PACK], F32, name="row_scale")
         ts_window = keep.tile([P, TABLE], F32, name="ts_window")
@@ -124,6 +126,9 @@ def tile_attend_gmf_sig_vu_kernel(tc, uT, vT, y, us, ts, offs, uoffs, out_0, out
             nc.vector.tensor_copy(x_planes[:, t, :], u_planes[t][:].indirect(u_list[:]))
             if t < last:
                 turn_images(t)
+        xq_r = mx_operand("xq_r", last * P, tag="u_plane%d" % last)
+        for cols in (slice(0, 2 * P), block(2)):
+            quantize(xq_r, E4M3, x_by_r, cols)
         x_by_d = keep.tile([P, LISTED, PACK], BF16, name="x_by_d", align_bytes=64)
         nc.scalar.copy(
             x_by_d[:].rearrange("p (j m) t -> p m j t", j=PACK),
@@ -139,9 +144,6 @@ def tile_attend_gmf_sig_vu_kernel(tc, uT, vT, y, us, ts, offs, uoffs, out_0, out
 
         for t in range(last):
             nc.vector.tensor_copy(w_by_d[:, :, t], v_planes[t][:].indirect(v_list[:]))
-            if t == 0:
-                xq_r = mx_operand("xq_r", tag="plane0")
-                quantize(xq_r, E4M3, x_by_r, slice(0, D))
             if t == 1:
                 xq_d = mx_operand("xq_d", tag="plane1")
                 quantize(xq_d, E4M3, x_by_d, slice(0, LISTED))
@@ -153,6 +155,8 @@ def tile_attend_gmf_sig_vu_kernel(tc, uT, vT, y, us, ts, offs, uoffs, out_0, out
             )
         for cols in (block(0), block(1), slice(half, LISTED)):
             quantize(wq_d, E4M3, w_by_d, cols)
+        xq_r_last = mx_operand("xq_r_last", P, tag="plane%d" % last)
+        quantize(xq_r_last, E4M3, x_by_r[:, block(last), :], block(0))
 
         padded = mx_operand("hq_r", half + LISTED)
         for part in padded:
@@ -193,7 +197,10 @@ def tile_attend_gmf_sig_vu_kernel(tc, uT, vT, y, us, ts, offs, uoffs, out_0, out
 
         def caption_grad(t, first, pool, tag):
             grad = pool.tile([P, LISTED], F32, name="dv", tag=tag)
-            matmul(grad[:], xq_r, block(t), hq_r, E5M2, everything)
+            if t < last:
+                matmul(grad[:], xq_r, block(t), hq_r, E5M2, everything)
+            else:
+                matmul(grad[:], xq_r_last, block(0), hq_r, E5M2, everything)
             dense = staged.tile([P, LISTED - first], F32, name="dense")
             nc.scalar.copy(dense[:], grad[:, first:])
             window = v_windows[t % V_WINDOWS]

@@ -9,8 +9,8 @@ D = 512
 LISTED = 512
 TABLE = 2048
 CHUNK = 128
-V_WINDOWS = 4
-U_WINDOWS = 3
+V_WINDOWS = 3
+U_WINDOWS = 2
 EARLY = 3
 
 FLOPS = 3 * 2 * D * LISTED * LISTED
@@ -247,6 +247,8 @@ def tile_attend_gmf_sig_vu_kernel(tc, uT, vT, y, us, ts, offs, uoffs, out_0, out
             )
         quantize(hq_i, E5M2, h_by_i, everything)
         caption_grad(EARLY - 1, half, turn_psum, "turn")
-        caption_grad(last, 0, turn_psum, "turn")
-        for t in range(PACK):
+        for t in range(U_WINDOWS):
+            image_grad(t)
+        caption_grad(last, 0, grad_psum, "grad")
+        for t in range(U_WINDOWS, PACK):
             image_grad(t)

@@ -12,6 +12,7 @@ CHUNK = 128
 V_WINDOWS = 3
 U_WINDOWS = 2
 EARLY = 3
+PIECES = 4
 
 FLOPS = 3 * 2 * D * LISTED * LISTED
 BYTES = 4 * (4 * D * TABLE + LISTED * LISTED + LISTED + TABLE) + 2 * 2 * P * (LISTED // 16)
@@ -24,6 +25,7 @@ U8 = mybir.dt.uint8
 E4M3 = mybir.dt.float8_e4m3fn_x4
 E5M2 = mybir.dt.float8_e5m2_x4
 MULT = mybir.AluOpType.mult
+COPY = mybir.ActivationFunctionType.Copy
 SIGMOID = mybir.ActivationFunctionType.Sigmoid
 
 
@@ -83,6 +85,9 @@ def tile_attend_gmf_sig_vu_kernel(tc, uT, vT, y, us, ts, offs, uoffs, out_0, out
         for t in range(PACK):
             nc.sync.dma_start(u_planes[t][:], u_rows[t])
 
+        warm = keep.tile([P, 8], F32, name="warm")
+        nc.vector.memset(warm[:, 0:1], 0.0)
+        nc.scalar.activation(warm[:, 1:2], warm[:, 0:1], SIGMOID)
         nc.vector.memset(ts_window[0 : P - 1, :], 0.0)
 
         ident_f32 = keep.tile([P, P], F32, name="ident_f32")
@@ -136,23 +141,27 @@ def tile_attend_gmf_sig_vu_kernel(tc, uT, vT, y, us, ts, offs, uoffs, out_0, out
         )
         turn_images(last)
         v_planes = [keep.tile([P, TABLE], F32, name="v_plane", tag="plane%d" % t, align_bytes=64) for t in range(PACK)]
-        for t in range(PACK):
+        first_planes = (last - 1, 0, 1)
+        for t in first_planes:
             nc.sync.dma_start(v_planes[t][:], v_rows[t])
+        pieces = [slice(k * TABLE // PIECES, (k + 1) * TABLE // PIECES) for k in range(PIECES)]
+        for cols in pieces:
+            nc.sync.dma_start(v_planes[last][:, cols], v_rows[last][:, cols])
 
         w_by_d = keep.tile([P, LISTED, PACK], BF16, name="w_by_d", align_bytes=64)
         wq_d = mx_operand("wq_d")
 
-        for t in range(last):
+        for t in first_planes:
             nc.vector.tensor_copy(w_by_d[:, :, t], v_planes[t][:].indirect(v_list[:]))
-            if t == 1:
-                xq_d = mx_operand("xq_d", tag="plane1")
+            if t == 0:
+                xq_d = mx_operand("xq_d", tag="plane0")
                 quantize(xq_d, E4M3, x_by_d, slice(0, LISTED))
         half = LISTED // 2
-        for n in range(2):
-            cols = slice(n * half, (n + 1) * half)
-            nc.vector.tensor_copy(
-                w_by_d[:, cols, last], v_planes[last][:].indirect(v_list[:, n * half // 16 : (n + 1) * half // 16])
-            )
+        v_last_bf16 = keep.tile([P, TABLE], BF16, name="v_last_bf16", tag="plane%d" % (last - 1), align_bytes=64)
+        for cols in pieces:
+            nc.scalar.activation(v_last_bf16[:, cols], v_planes[last][:, cols], COPY)
+        nc.vector.tensor_copy(w_by_d[:, 0:half, last], v_planes[last][:].indirect(v_list[:, 0 : half // 16]))
+        nc.scalar.activation(w_by_d[:, half:, last], v_last_bf16[:].indirect(v_list[:, half // 16 :]), COPY)
         for cols in (block(0), block(1), slice(half, LISTED)):
             quantize(wq_d, E4M3, w_by_d, cols)
         xq_r_last = mx_operand("xq_r_last", P, tag="plane%d" % last)

@@ -68,13 +68,13 @@ def tile_attend_gmf_sig_vu_kernel(tc, uT, vT, y, us, ts, offs, uoffs, out_0, out
 
         u_list = keep.tile([P, LISTED // 16], U16, name="u_list")
         v_list = keep.tile([P, LISTED // 16], U16, name="v_list")
-        u_planes = [
-            keep.tile([P, TABLE], F32, name="u_plane%d" % t, tag="u_plane%d" % t, align_bytes=64) for t in range(PACK)
+        u_pairs = [
+            keep.tile([P, 2, TABLE], F32, name="u_pair%d" % n, tag="u_pair%d" % n, align_bytes=64) for n in range(2)
         ]
         labels = keep.tile([P, PACK, LISTED], F32, name="labels")
         row_scale = keep.tile([P, PACK], F32, name="row_scale")
         ts_window = keep.tile([P, TABLE], F32, name="ts_window")
-        u_rows = uT.rearrange("(p t) c -> t p c", t=PACK)
+        u_rows = uT.rearrange("(p n e) c -> n p e c", n=2, e=2)
         v_rows = vT.rearrange("(p t) c -> t p c", t=PACK)
 
         nc.scalar.dma_start(ts_window[P - 1 : P, :], ts[0:1, :])
@@ -82,8 +82,8 @@ def tile_attend_gmf_sig_vu_kernel(tc, uT, vT, y, us, ts, offs, uoffs, out_0, out
         nc.sync.dma_start(labels[:], y.rearrange("b (p t) i -> p (b t) i", t=PACK))
         nc.sync.dma_start(v_list[:], offs)
         nc.sync.dma_start(u_list[:], uoffs)
-        for t in range(PACK):
-            nc.sync.dma_start(u_planes[t][:], u_rows[t])
+        for n in range(2):
+            nc.sync.dma_start(u_pairs[n][:], u_rows[n])
 
         warm = keep.tile([P, 8], F32, name="warm")
         nc.vector.memset(warm[:, 0:1], 0.0)
@@ -128,10 +128,10 @@ def tile_attend_gmf_sig_vu_kernel(tc, uT, vT, y, us, ts, offs, uoffs, out_0, out
             nc.scalar.copy(x_by_r[:, block(t), :], turned[:].rearrange("m j p -> m p j"))
 
         for t in range(PACK):
-            nc.vector.tensor_copy(x_planes[:, t, :], u_planes[t][:].indirect(u_list[:]))
+            nc.vector.tensor_copy(x_planes[:, t, :], u_pairs[t // 2][:, t % 2, :].indirect(u_list[:]))
             if t < last:
                 turn_images(t)
-        xq_r = mx_operand("xq_r", last * P, tag="u_plane%d" % last)
+        xq_r = mx_operand("xq_r", last * P, tag="u_pair1")
         for cols in (slice(0, 2 * P), block(2)):
             quantize(xq_r, E4M3, x_by_r, cols)
         x_by_d = keep.tile([P, LISTED, PACK], BF16, name="x_by_d", align_bytes=64)

@@ -33,10 +33,10 @@ def tile_attend_gmf_sig_vu_kernel(tc, uT, vT, y, us, ts, offs, uoffs, out_0, out
     nc = tc.nc
     with ExitStack() as ctx:
         keep = ctx.enter_context(tc.tile_pool(name="keep", bufs=1))
-        work = ctx.enter_context(tc.tile_pool(name="work", bufs=3))
+        work = ctx.enter_context(tc.tile_pool(name="work", bufs=2))
         staged = ctx.enter_context(tc.tile_pool(name="staged", bufs=6))
         turn_psum = ctx.enter_context(tc.psum_pool(name="turn_psum", bufs=2))
-        score_psum = ctx.enter_context(tc.psum_pool(name="score_psum", bufs=4))
+        score_psum = ctx.enter_context(tc.psum_pool(name="score_psum", bufs=1))
         grad_psum = ctx.enter_context(tc.psum_pool(name="grad_psum", bufs=2))
 
         def mx_operand(name, width=LISTED, tag=""):
@@ -172,24 +172,28 @@ def tile_attend_gmf_sig_vu_kernel(tc, uT, vT, y, us, ts, offs, uoffs, out_0, out
             nc.gpsimd.memset(part[:, 0:half], 0)
         hq_r = [part[:, half:] for part in padded]
         chunks = LISTED // CHUNK
-        probs = []
+        scores = []
         for c in range(chunks):
-            score = score_psum.tile([P, PACK, CHUNK], F32, name="score", tag="score")
+            score = score_psum.tile([P, PACK, CHUNK], F32, name="score", tag="score%d" % c)
             for t in range(PACK):
                 matmul(score[:, t, :], xq_d, block(t), wq_d, E4M3, block(c))
-            if c < chunks - 1:
-                logit = work.tile([P, PACK, CHUNK], F32, name="logit")
-            else:
-                logit = keep.tile([P, PACK, CHUNK], F32, name="last_logit", tag="w_by_i", align_bytes=64)
-            nc.vector.tensor_tensor(logit[:], score[:], q_planes[:, :, block(c)], MULT)
-            prob = keep.tile([P, CHUNK, PACK], F32, name="prob%d" % c)
-            nc.scalar.activation(prob[:], logit[:].rearrange("p t i -> p i t"), SIGMOID)
-            probs.append(prob)
-        h = keep.tile([P, LISTED, PACK], BF16, name="h", tag="q_planes", align_bytes=64)
-        for c in range(chunks):
+            scores.append(score)
+        h = keep.tile([P, LISTED, PACK], BF16, name="h", align_bytes=64)
+
+        def sigmoid_of(c, logit):
+            nc.vector.tensor_tensor(logit, scores[c][:], q_planes[:, :, block(c)], MULT)
+            prob = keep.tile([P, CHUNK, PACK], F32, name="prob", tag="prob%d" % c, align_bytes=64)
+            nc.scalar.activation(prob[:], logit.rearrange("p t i -> p i t"), SIGMOID)
+            return prob
+
+        probs = []
+        for c in range(chunks // 2):
+            logit = work.tile([P, PACK, CHUNK], F32, name="logit")
+            probs.append(sigmoid_of(c, logit[:]))
+        for c in range(chunks // 2):
             nc.vector.tensor_tensor(h[:, block(c), :], probs[c][:], q[:, block(c), :], MULT)
-            if c >= 2:
-                quantize(hq_r, E5M2, h, slice((c - 2) * half, (c - 1) * half))
+        for c in range(chunks // 2):
+            quantize(hq_r, E5M2, h, block(c))
 
         h_by_i = keep.tile([P, LISTED, PACK], BF16, name="h_by_i", align_bytes=64)
         hq_i = mx_operand("hq_i")
@@ -200,7 +204,10 @@ def tile_attend_gmf_sig_vu_kernel(tc, uT, vT, y, us, ts, offs, uoffs, out_0, out
         def early_caption_grad(t):
             grad = grad_psum.tile([P, LISTED], F32, name="dv", tag="grad")
             matmul(grad[:], xq_r, block(t), padded, E5M2, everything)
-            dense = staged.tile([P, half], F32, name="dense")
+            if t < EARLY - 1:
+                dense = staged.tile([P, half], F32, name="dense")
+            else:
+                dense = keep.tile([P, half], F32, name="late_dense", tag="prob%d" % (chunks - 1), align_bytes=64)
             nc.scalar.copy(dense[:], grad[:, half:])
             nc.vector.tensor_copy(v_windows[t][:].indirect(v_list[:, 0 : half // 16]), dense[:])
 
@@ -229,12 +236,18 @@ def tile_attend_gmf_sig_vu_kernel(tc, uT, vT, y, us, ts, offs, uoffs, out_0, out
                 nc.sync.dma_start(du_rows[t][:, 0 : TABLE // 2], window[:, 0 : TABLE // 2])
                 nc.scalar.dma_start(du_rows[t][:, TABLE // 2 :], window[:, TABLE // 2 :])
 
-        for t in range(EARLY):
-            early_caption_grad(t)
-        w_by_i = keep.tile([P, D, PACK], BF16, name="w_by_i", tag="w_by_i", align_bytes=64)
+        early_caption_grad(0)
+        late_logits = keep.tile([P, chunks // 2, PACK, CHUNK], F32, name="late_logits", tag="prob1", align_bytes=64)
+        for c in range(chunks // 2, chunks):
+            prob = sigmoid_of(c, late_logits[:, c - chunks // 2])
+            nc.gpsimd.tensor_tensor(h[:, block(c), :], prob[:], q[:, block(c), :], MULT)
+        early_caption_grad(1)
+        quantize(hq_r, E5M2, h, slice(half, LISTED))
+        early_caption_grad(2)
+        w_by_i = keep.tile([P, D, PACK], BF16, name="w_by_i", tag="prob1", align_bytes=64)
         w_words = w_by_d[:].rearrange("p i t -> p (i t)").bitcast(F32)
         for u in range(2):
-            turned = score_psum.tile([P, PACK, P], F32, name="w_turned", tag="score")
+            turned = score_psum.tile([P, PACK, P], F32, name="w_turned", tag="score%d" % (chunks // 2 + u))
             for j in range(PACK):
                 nc.tensor.transpose(turned[:, j, :], w_words[:, 2 * j + u : 2 * LISTED : 2 * PACK], ident_f32[:])
             nc.scalar.copy(

@@ -71,7 +71,10 @@ def tile_attend_gmf_sig_vu_kernel(tc, uT, vT, y, us, ts, offs, uoffs, out_0, out
         u_pairs = [
             keep.tile([P, 2, TABLE], F32, name="u_pair%d" % n, tag="u_pair%d" % n, align_bytes=64) for n in range(2)
         ]
-        labels = keep.tile([P, PACK, LISTED], F32, name="labels")
+        half = LISTED // 2
+        labels = [
+            keep.tile([P, PACK, half], F32, name="labels%d" % n, tag="labels%d" % n, align_bytes=64) for n in range(2)
+        ]
         row_scale = keep.tile([P, PACK], F32, name="row_scale")
         ts_window = keep.tile([P, TABLE], F32, name="ts_window")
         u_rows = uT.rearrange("(p n e) c -> n p e c", n=2, e=2)
@@ -79,11 +82,10 @@ def tile_attend_gmf_sig_vu_kernel(tc, uT, vT, y, us, ts, offs, uoffs, out_0, out
 
         nc.scalar.dma_start(ts_window[P - 1 : P, :], ts[0:1, :])
         nc.scalar.dma_start(row_scale[:], us.rearrange("b (p t) o -> p (b t o)", t=PACK))
-        nc.sync.dma_start(labels[:], y.rearrange("b (p t) i -> p (b t) i", t=PACK))
         nc.sync.dma_start(v_list[:], offs)
+        nc.sync.dma_start(u_pairs[0][:], u_rows[0])
         nc.sync.dma_start(u_list[:], uoffs)
-        for n in range(2):
-            nc.sync.dma_start(u_pairs[n][:], u_rows[n])
+        nc.sync.dma_start(u_pairs[1][:], u_rows[1])
 
         warm = keep.tile([P, 8], F32, name="warm")
         nc.vector.memset(warm[:, 0:1], 0.0)
@@ -103,19 +105,15 @@ def tile_attend_gmf_sig_vu_kernel(tc, uT, vT, y, us, ts, offs, uoffs, out_0, out
         ts_turned = turn_psum.tile([P, PACK, P], F32, name="ts_turned", tag="turn")
         for k in range(PACK):
             nc.tensor.transpose(ts_turned[:, k, :], ts_listed[:, block(k)], ident_f32[:])
-        neg_ts = keep.tile([P, PACK], F32, name="neg_ts", tag="x_planes")
-        nc.vector.tensor_scalar(neg_ts[:], ts_turned[:, :, P - 1], -1.0, None, MULT)
+        neg_ts = keep.tile([P, PACK], F32, name="neg_ts")
+        nc.scalar.activation(neg_ts[:], ts_turned[:, :, P - 1], COPY, scale=-1.0)
         neg_ts_rows = grad_psum.tile([P, LISTED], F32, name="neg_ts_rows", tag="grad")
         for k in range(PACK):
             nc.tensor.transpose(neg_ts_rows[:, block(k)], neg_ts[:, k : k + 1].to_broadcast([P, P]), ident_f32[:])
 
-        q_planes = keep.tile([P, PACK, LISTED], F32, name="q_planes", tag="q_planes", align_bytes=64)
+        neg_scale = keep.tile([P, PACK, LISTED], F32, name="neg_scale")
         for t in range(PACK):
-            nc.vector.scalar_tensor_tensor(
-                q_planes[:, t, :], labels[:, t, :], row_scale[:, t : t + 1], neg_ts_rows[:], MULT, MULT
-            )
-        q = keep.tile([P, LISTED, PACK], F32, name="q")
-        nc.scalar.copy(q[:], q_planes[:].rearrange("p t i -> p i t"))
+            nc.scalar.activation(neg_scale[:, t, :], neg_ts_rows[:], COPY, scale=row_scale[:, t : t + 1])
 
         x_planes = keep.tile([P, PACK, LISTED], F32, name="x_planes", tag="x_planes")
         x_by_r = keep.tile([P, D, PACK], BF16, name="x_by_r", align_bytes=64)
@@ -147,52 +145,69 @@ def tile_attend_gmf_sig_vu_kernel(tc, uT, vT, y, us, ts, offs, uoffs, out_0, out
         pieces = [slice(k * TABLE // PIECES, (k + 1) * TABLE // PIECES) for k in range(PIECES)]
         for cols in pieces:
             nc.sync.dma_start(v_planes[last][:, cols], v_rows[last][:, cols])
+        y_rows = y.rearrange("b (p t) i -> p (b t) i", t=PACK)
+        for n in range(2):
+            nc.sync.dma_start(labels[n][:], y_rows[:, :, n * half : (n + 1) * half])
 
         w_by_d = keep.tile([P, LISTED, PACK], BF16, name="w_by_d", align_bytes=64)
-        wq_d = mx_operand("wq_d")
+        wq_d = mx_operand("wq_d", half)
 
         for t in first_planes:
             nc.vector.tensor_copy(w_by_d[:, :, t], v_planes[t][:].indirect(v_list[:]))
             if t == 0:
                 xq_d = mx_operand("xq_d", tag="plane0")
                 quantize(xq_d, E4M3, x_by_d, slice(0, LISTED))
-        half = LISTED // 2
         v_last_bf16 = keep.tile([P, TABLE], BF16, name="v_last_bf16", tag="plane%d" % (last - 1), align_bytes=64)
         for cols in pieces:
             nc.scalar.activation(v_last_bf16[:, cols], v_planes[last][:, cols], COPY)
         nc.vector.tensor_copy(w_by_d[:, 0:half, last], v_planes[last][:].indirect(v_list[:, 0 : half // 16]))
         nc.scalar.activation(w_by_d[:, half:, last], v_last_bf16[:].indirect(v_list[:, half // 16 :]), COPY)
-        for cols in (block(0), block(1), slice(half, LISTED)):
-            quantize(wq_d, E4M3, w_by_d, cols)
-        xq_r_last = mx_operand("xq_r_last", P, tag="plane%d" % last)
-        quantize(xq_r_last, E4M3, x_by_r[:, block(last), :], block(0))
+        for c in range(2):
+            quantize(wq_d, E4M3, w_by_d, block(c))
 
         padded = mx_operand("hq_r", half + LISTED)
         for part in padded:
             nc.gpsimd.memset(part[:, 0:half], 0)
         hq_r = [part[:, half:] for part in padded]
         chunks = LISTED // CHUNK
-        scores = []
-        for c in range(chunks):
-            score = score_psum.tile([P, PACK, CHUNK], F32, name="score", tag="score%d" % c)
-            for t in range(PACK):
-                matmul(score[:, t, :], xq_d, block(t), wq_d, E4M3, block(c))
-            scores.append(score)
         h = keep.tile([P, LISTED, PACK], BF16, name="h", align_bytes=64)
 
-        def sigmoid_of(c, logit):
-            nc.vector.tensor_tensor(logit, scores[c][:], q_planes[:, :, block(c)], MULT)
+        def scores_of(c, captions):
+            score = score_psum.tile([P, PACK, CHUNK], F32, name="score", tag="score%d" % c)
+            for t in range(PACK):
+                matmul(score[:, t, :], xq_d, block(t), captions, E4M3, block(c % 2))
+            return score
+
+        def factor_of(c, q):
+            nc.vector.tensor_tensor(
+                q.rearrange("p (g i) t -> p g t i", i=2),
+                labels[c // 2][:, :, block(c % 2)].rearrange("p t (g i) -> p g t i", i=2),
+                neg_scale[:, :, block(c)].rearrange("p t (g i) -> p g t i", i=2),
+                MULT,
+            )
+
+        def sigmoid_of(c, score, q, logit):
+            nc.vector.tensor_tensor(logit, score[:].rearrange("p t i -> p i t"), q, MULT)
             prob = keep.tile([P, CHUNK, PACK], F32, name="prob", tag="prob%d" % c, align_bytes=64)
-            nc.scalar.activation(prob[:], logit.rearrange("p t i -> p i t"), SIGMOID)
+            nc.scalar.activation(prob[:], logit, SIGMOID)
             return prob
 
+        scores = [scores_of(c, wq_d) for c in range(2)]
+        q_first = keep.tile([P, 2, CHUNK, PACK], F32, name="q_first")
+        for c in range(2):
+            factor_of(c, q_first[:, c])
         probs = []
-        for c in range(chunks // 2):
-            logit = work.tile([P, PACK, CHUNK], F32, name="logit")
-            probs.append(sigmoid_of(c, logit[:]))
-        for c in range(chunks // 2):
-            nc.vector.tensor_tensor(h[:, block(c), :], probs[c][:], q[:, block(c), :], MULT)
-        for c in range(chunks // 2):
+        for c in range(2):
+            logit = work.tile([P, CHUNK, PACK], F32, name="logit")
+            probs.append(sigmoid_of(c, scores[c], q_first[:, c], logit[:]))
+        wq_d_late = mx_operand("wq_d_late", half, tag="labels0")
+        quantize(wq_d_late, E4M3, w_by_d[:, half:, :], slice(0, half))
+        late_scores = [scores_of(c, wq_d_late) for c in range(2, chunks)]
+        xq_r_last = mx_operand("xq_r_last", P, tag="plane%d" % last)
+        quantize(xq_r_last, E4M3, x_by_r[:, block(last), :], block(0))
+        for c in range(2):
+            nc.vector.tensor_tensor(h[:, block(c), :], probs[c][:], q_first[:, c], MULT)
+        for c in range(2):
             quantize(hq_r, E5M2, h, block(c))
 
         h_by_i = keep.tile([P, LISTED, PACK], BF16, name="h_by_i", align_bytes=64)
@@ -209,6 +224,9 @@ def tile_attend_gmf_sig_vu_kernel(tc, uT, vT, y, us, ts, offs, uoffs, out_0, out
             else:
                 dense = keep.tile([P, half], F32, name="late_dense", tag="prob%d" % (chunks - 1), align_bytes=64)
             nc.scalar.copy(dense[:], grad[:, half:])
+            return dense
+
+        def early_scatter(t, dense):
             nc.vector.tensor_copy(v_windows[t][:].indirect(v_list[:, 0 : half // 16]), dense[:])
 
         def caption_grad(t, first, pool, tag):
@@ -236,15 +254,19 @@ def tile_attend_gmf_sig_vu_kernel(tc, uT, vT, y, us, ts, offs, uoffs, out_0, out
                 nc.sync.dma_start(du_rows[t][:, 0 : TABLE // 2], window[:, 0 : TABLE // 2])
                 nc.scalar.dma_start(du_rows[t][:, TABLE // 2 :], window[:, TABLE // 2 :])
 
-        early_caption_grad(0)
-        late_logits = keep.tile([P, chunks // 2, PACK, CHUNK], F32, name="late_logits", tag="prob1", align_bytes=64)
-        for c in range(chunks // 2, chunks):
-            prob = sigmoid_of(c, late_logits[:, c - chunks // 2])
-            nc.gpsimd.tensor_tensor(h[:, block(c), :], prob[:], q[:, block(c), :], MULT)
-        early_caption_grad(1)
+        first_dense = early_caption_grad(0)
+        q_late = keep.tile([P, 2, CHUNK, PACK], F32, name="q_late", tag="prob1", align_bytes=64)
+        for n in range(2):
+            factor_of(2 + n, q_late[:, n])
+        late_logits = keep.tile([P, 2, CHUNK, PACK], F32, name="late_logits", tag="late_logits", align_bytes=64)
+        for n in range(2):
+            prob = sigmoid_of(2 + n, late_scores[n], q_late[:, n], late_logits[:, n])
+            nc.gpsimd.tensor_tensor(h[:, block(2 + n), :], prob[:], q_late[:, n], MULT)
+        early_scatter(0, first_dense)
+        early_scatter(1, early_caption_grad(1))
         quantize(hq_r, E5M2, h, slice(half, LISTED))
-        early_caption_grad(2)
-        w_by_i = keep.tile([P, D, PACK], BF16, name="w_by_i", tag="prob1", align_bytes=64)
+        early_scatter(2, early_caption_grad(2))
+        w_by_i = keep.tile([P, D, PACK], BF16, name="w_by_i", tag="late_logits", align_bytes=64)
         w_words = w_by_d[:].rearrange("p i t -> p (i t)").bitcast(F32)
         for u in range(2):
             turned = score_psum.tile([P, PACK, P], F32, name="w_turned", tag="score%d" % (chunks // 2 + u))

@@ -12,7 +12,7 @@ CHUNK = 128
 V_WINDOWS = 3
 U_WINDOWS = 2
 EARLY = 3
-PIECES = 4
+PIECES = 2
 
 FLOPS = 3 * 2 * D * LISTED * LISTED
 BYTES = 4 * (4 * D * TABLE + LISTED * LISTED + LISTED + TABLE) + 2 * 2 * P * (LISTED // 16)
@@ -68,24 +68,25 @@ def tile_attend_gmf_sig_vu_kernel(tc, uT, vT, y, us, ts, offs, uoffs, out_0, out
 
         u_list = keep.tile([P, LISTED // 16], U16, name="u_list")
         v_list = keep.tile([P, LISTED // 16], U16, name="v_list")
-        u_pairs = [
-            keep.tile([P, 2, TABLE], F32, name="u_pair%d" % n, tag="u_pair%d" % n, align_bytes=64) for n in range(2)
-        ]
+        u_pair = keep.tile([P, 2, TABLE], F32, name="u_pair")
+        u_late = [keep.tile([P, TABLE], F32, name="u_late", tag="u_late%d" % n, align_bytes=64) for n in range(2)]
+        u_planes = [u_pair[:, 0, :], u_pair[:, 1, :], u_late[0][:], u_late[1][:]]
         half = LISTED // 2
         labels = [
             keep.tile([P, PACK, half], F32, name="labels%d" % n, tag="labels%d" % n, align_bytes=64) for n in range(2)
         ]
         row_scale = keep.tile([P, PACK], F32, name="row_scale")
         ts_window = keep.tile([P, TABLE], F32, name="ts_window")
-        u_rows = uT.rearrange("(p n e) c -> n p e c", n=2, e=2)
+        u_rows = uT.rearrange("(p t) c -> p t c", t=PACK)
         v_rows = vT.rearrange("(p t) c -> t p c", t=PACK)
 
         nc.scalar.dma_start(ts_window[P - 1 : P, :], ts[0:1, :])
         nc.scalar.dma_start(row_scale[:], us.rearrange("b (p t) o -> p (b t o)", t=PACK))
         nc.sync.dma_start(v_list[:], offs)
-        nc.sync.dma_start(u_pairs[0][:], u_rows[0])
+        nc.sync.dma_start(u_pair[:], u_rows[:, 0:2, :])
         nc.sync.dma_start(u_list[:], uoffs)
-        nc.sync.dma_start(u_pairs[1][:], u_rows[1])
+        for n in range(2):
+            nc.sync.dma_start(u_late[n][:], u_rows[:, 2 + n, :])
 
         warm = keep.tile([P, 8], F32, name="warm")
         nc.vector.memset(warm[:, 0:1], 0.0)
@@ -126,10 +127,10 @@ def tile_attend_gmf_sig_vu_kernel(tc, uT, vT, y, us, ts, offs, uoffs, out_0, out
             nc.scalar.copy(x_by_r[:, block(t), :], turned[:].rearrange("m j p -> m p j"))
 
         for t in range(PACK):
-            nc.vector.tensor_copy(x_planes[:, t, :], u_pairs[t // 2][:, t % 2, :].indirect(u_list[:]))
+            nc.vector.tensor_copy(x_planes[:, t, :], u_planes[t].indirect(u_list[:]))
             if t < last:
                 turn_images(t)
-        xq_r = mx_operand("xq_r", last * P, tag="u_pair1")
+        xq_r = mx_operand("xq_r", last * P, tag="u_late1")
         for cols in (slice(0, 2 * P), block(2)):
             quantize(xq_r, E4M3, x_by_r, cols)
         x_by_d = keep.tile([P, LISTED, PACK], BF16, name="x_by_d", align_bytes=64)
@@ -155,8 +156,11 @@ def tile_attend_gmf_sig_vu_kernel(tc, uT, vT, y, us, ts, offs, uoffs, out_0, out
         for t in first_planes:
             nc.vector.tensor_copy(w_by_d[:, :, t], v_planes[t][:].indirect(v_list[:]))
             if t == 0:
-                xq_d = mx_operand("xq_d", tag="plane0")
+                xq_late = mx_operand("xq_late", LISTED + P, tag="plane0")
+                xq_d = [part[:, 0:LISTED] for part in xq_late]
+                xq_r_last = [part[:, LISTED:] for part in xq_late]
                 quantize(xq_d, E4M3, x_by_d, slice(0, LISTED))
+                quantize(xq_r_last, E4M3, x_by_r[:, block(last), :], block(0))
         v_last_bf16 = keep.tile([P, TABLE], BF16, name="v_last_bf16", tag="plane%d" % (last - 1), align_bytes=64)
         for cols in pieces:
             nc.scalar.activation(v_last_bf16[:, cols], v_planes[last][:, cols], COPY)
@@ -203,8 +207,8 @@ def tile_attend_gmf_sig_vu_kernel(tc, uT, vT, y, us, ts, offs, uoffs, out_0, out
         wq_d_late = mx_operand("wq_d_late", half, tag="labels0")
         quantize(wq_d_late, E4M3, w_by_d[:, half:, :], slice(0, half))
         late_scores = [scores_of(c, wq_d_late) for c in range(2, chunks)]
-        xq_r_last = mx_operand("xq_r_last", P, tag="plane%d" % last)
-        quantize(xq_r_last, E4M3, x_by_r[:, block(last), :], block(0))
+        q_third = keep.tile([P, CHUNK, PACK], F32, name="q_third")
+        factor_of(2, q_third[:])
         for c in range(2):
             nc.vector.tensor_tensor(h[:, block(c), :], probs[c][:], q_first[:, c], MULT)
         for c in range(2):
@@ -255,13 +259,14 @@ def tile_attend_gmf_sig_vu_kernel(tc, uT, vT, y, us, ts, offs, uoffs, out_0, out
                 nc.scalar.dma_start(du_rows[t][:, TABLE // 2 :], window[:, TABLE // 2 :])
 
         first_dense = early_caption_grad(0)
-        q_late = keep.tile([P, 2, CHUNK, PACK], F32, name="q_late", tag="prob1", align_bytes=64)
+        behind_h = keep.tile([P, 2, CHUNK, PACK], F32, name="behind_h", tag="prob1", align_bytes=64)
+        last_logit = keep.tile([P, CHUNK, PACK], F32, name="last_logit", tag="late_logits", align_bytes=64)
+        factor_of(3, behind_h[:, 1])
+        q_late = [q_third[:], behind_h[:, 1]]
+        late_logits = [behind_h[:, 0], last_logit[:]]
         for n in range(2):
-            factor_of(2 + n, q_late[:, n])
-        late_logits = keep.tile([P, 2, CHUNK, PACK], F32, name="late_logits", tag="late_logits", align_bytes=64)
-        for n in range(2):
-            prob = sigmoid_of(2 + n, late_scores[n], q_late[:, n], late_logits[:, n])
-            nc.gpsimd.tensor_tensor(h[:, block(2 + n), :], prob[:], q_late[:, n], MULT)
+            prob = sigmoid_of(2 + n, late_scores[n], q_late[n], late_logits[n])
+            nc.gpsimd.tensor_tensor(h[:, block(2 + n), :], prob[:], q_late[n], MULT)
         early_scatter(0, first_dense)
         early_scatter(1, early_caption_grad(1))
         quantize(hq_r, E5M2, h, slice(half, LISTED))

@@ -33,7 +33,6 @@ def tile_attend_gmf_sig_vu_kernel(tc, uT, vT, y, us, ts, offs, uoffs, out_0, out
     nc = tc.nc
     with ExitStack() as ctx:
         keep = ctx.enter_context(tc.tile_pool(name="keep", bufs=1))
-        work = ctx.enter_context(tc.tile_pool(name="work", bufs=2))
         staged = ctx.enter_context(tc.tile_pool(name="staged", bufs=6))
         turn_psum = ctx.enter_context(tc.psum_pool(name="turn_psum", bufs=2))
         score_psum = ctx.enter_context(tc.psum_pool(name="score_psum", bufs=1))
@@ -202,7 +201,7 @@ def tile_attend_gmf_sig_vu_kernel(tc, uT, vT, y, us, ts, offs, uoffs, out_0, out
             factor_of(c, q_first[:, c])
         probs = []
         for c in range(2):
-            logit = work.tile([P, CHUNK, PACK], F32, name="logit")
+            logit = keep.tile([P, CHUNK, PACK], F32, name="logit", tag="logit%d" % c, align_bytes=64)
             probs.append(sigmoid_of(c, scores[c], q_first[:, c], logit[:]))
         wq_d_late = mx_operand("wq_d_late", half, tag="labels0")
         quantize(wq_d_late, E4M3, w_by_d[:, half:, :], slice(0, half))
@@ -214,7 +213,7 @@ def tile_attend_gmf_sig_vu_kernel(tc, uT, vT, y, us, ts, offs, uoffs, out_0, out
         for c in range(2):
             quantize(hq_r, E5M2, h, block(c))
 
-        h_by_i = keep.tile([P, LISTED, PACK], BF16, name="h_by_i", align_bytes=64)
+        h_by_i = keep.tile([P, LISTED, PACK], BF16, name="h_by_i", tag="h_by_i", align_bytes=64)
         hq_i = mx_operand("hq_i")
         dv_rows = out_0.rearrange("(p t) c -> t p c", t=PACK)
         du_rows = out_1.rearrange("(p t) c -> t p c", t=PACK)
@@ -241,16 +240,16 @@ def tile_attend_gmf_sig_vu_kernel(tc, uT, vT, y, us, ts, offs, uoffs, out_0, out
                 matmul(grad[:], xq_r_last, block(0), hq_r, E5M2, everything)
             dense = staged.tile([P, LISTED - first], F32, name="dense")
             nc.scalar.copy(dense[:], grad[:, first:])
-            window = v_windows[t % V_WINDOWS]
+            window = v_windows[t]
             nc.vector.tensor_copy(window[:].indirect(v_list[:, first // 16 :]), dense[:])
             nc.sync.dma_start(dv_rows[t], window[:])
 
         def image_grad(t):
             grad = grad_psum.tile([P, LISTED], F32, name="du", tag="grad")
-            matmul(grad[:], wq_i, block(t), hq_i, E5M2, everything)
+            matmul(grad[:], wq_i[t // 2], block(t % 2), hq_i, E5M2, everything)
             dense = staged.tile([P, LISTED], F32, name="dense")
             nc.scalar.copy(dense[:], grad[:])
-            window = u_windows[t % U_WINDOWS]
+            window = u_windows[t % (U_WINDOWS + 1)]
             nc.vector.tensor_copy(window[:].indirect(u_list[:]), dense[:])
             if t < last:
                 nc.sync.dma_start(du_rows[t], window[:])
@@ -271,23 +270,29 @@ def tile_attend_gmf_sig_vu_kernel(tc, uT, vT, y, us, ts, offs, uoffs, out_0, out
         early_scatter(1, early_caption_grad(1))
         quantize(hq_r, E5M2, h, slice(half, LISTED))
         early_scatter(2, early_caption_grad(2))
-        w_by_i = keep.tile([P, D, PACK], BF16, name="w_by_i", tag="late_logits", align_bytes=64)
+        w_by_i = [
+            keep.tile([P, 2 * P, PACK], BF16, name="w_by_i", tag=tag, align_bytes=64) for tag in ("logit1", "late_logits")
+        ]
         w_words = w_by_d[:].rearrange("p i t -> p (i t)").bitcast(F32)
         for u in range(2):
-            turned = score_psum.tile([P, PACK, P], F32, name="w_turned", tag="score%d" % (chunks // 2 + u))
+            turned = score_psum.tile([P, PACK, P], F32, name="w_turned", tag="score%d" % (u * (chunks - 1)))
             for j in range(PACK):
                 nc.tensor.transpose(turned[:, j, :], w_words[:, 2 * j + u : 2 * LISTED : 2 * PACK], ident_f32[:])
             nc.scalar.copy(
-                w_by_i[:].rearrange("m (u e p) j -> m u e p j", u=2, e=2)[:, u],
+                w_by_i[u][:].rearrange("m (e p) j -> m e p j", e=2),
                 turned[:].rearrange("m j p -> m (j p)").bitcast(BF16).rearrange("m (j p e) -> m e p j", j=PACK, e=2),
             )
-        wq_i = mx_operand("wq_i")
-        quantize(wq_i, E4M3, w_by_i, everything)
+        wq_i = [mx_operand("wq_i%d" % u, half, tag=tag) for u, tag in enumerate(("prob2", "prob1"))]
+        for u in range(2):
+            quantize(wq_i[u], E4M3, w_by_i[u], slice(0, half))
+        v_windows.append(keep.tile([P, TABLE], F32, name="v_window3", tag="late_logits", align_bytes=64))
+        nc.gpsimd.memset(v_windows[V_WINDOWS][:], 0.0)
         for t in range(EARLY - 1):
             caption_grad(t, half, grad_psum, "grad")
+        caption_grad(EARLY - 1, half, turn_psum, "turn")
         h_words = h[:].rearrange("p i t -> p (i t)").bitcast(F32)
         for u in range(2):
-            turned = turn_psum.tile([P, PACK, P], F32, name="h_turned", tag="turn")
+            turned = grad_psum.tile([P, PACK, P], F32, name="h_turned", tag="grad")
             for j in range(PACK):
                 nc.tensor.transpose(turned[:, j, :], h_words[:, 2 * j + u : 2 * LISTED : 2 * PACK], ident_f32[:])
             nc.scalar.copy(
@@ -295,9 +300,8 @@ def tile_attend_gmf_sig_vu_kernel(tc, uT, vT, y, us, ts, offs, uoffs, out_0, out
                 turned[:].rearrange("m j p -> m (j p)").bitcast(BF16).rearrange("m (j p e) -> m p e j", j=PACK, e=2),
             )
         quantize(hq_i, E5M2, h_by_i, everything)
-        caption_grad(EARLY - 1, half, turn_psum, "turn")
-        for t in range(U_WINDOWS):
-            image_grad(t)
+        u_windows.append(keep.tile([P, TABLE], F32, name="u_window2", tag="h_by_i", align_bytes=64))
+        nc.gpsimd.memset(u_windows[U_WINDOWS][:], 0.0)
         caption_grad(last, 0, grad_psum, "grad")
-        for t in range(U_WINDOWS, PACK):
+        for t in range(PACK):
             image_grad(t)

@@ -251,11 +251,7 @@ def tile_attend_gmf_sig_vu_kernel(tc, uT, vT, y, us, ts, offs, uoffs, out_0, out
             nc.scalar.copy(dense[:], grad[:])
             window = u_windows[t % (U_WINDOWS + 1)]
             nc.vector.tensor_copy(window[:].indirect(u_list[:]), dense[:])
-            if t < last:
-                nc.sync.dma_start(du_rows[t], window[:])
-            else:
-                nc.sync.dma_start(du_rows[t][:, 0 : TABLE // 2], window[:, 0 : TABLE // 2])
-                nc.scalar.dma_start(du_rows[t][:, TABLE // 2 :], window[:, TABLE // 2 :])
+            nc.sync.dma_start(du_rows[t], window[:])
 
         first_dense = early_caption_grad(0)
         behind_h = keep.tile([P, 2, CHUNK, PACK], F32, name="behind_h", tag="prob1", align_bytes=64)

@@ -196,7 +196,7 @@ def tile_attend_gmf_sig_vu_kernel(tc, uT, vT, y, us, ts, offs, uoffs, out_0, out
             return prob
 
         scores = [scores_of(c, wq_d) for c in range(2)]
-        q_first = keep.tile([P, 2, CHUNK, PACK], F32, name="q_first")
+        q_first = keep.tile([P, 2, CHUNK, PACK], F32, name="q_first", tag="q_first", align_bytes=64)
         for c in range(2):
             factor_of(c, q_first[:, c])
         probs = []
@@ -256,31 +256,32 @@ def tile_attend_gmf_sig_vu_kernel(tc, uT, vT, y, us, ts, offs, uoffs, out_0, out
         first_dense = early_caption_grad(0)
         behind_h = keep.tile([P, 2, CHUNK, PACK], F32, name="behind_h", tag="prob1", align_bytes=64)
         last_logit = keep.tile([P, CHUNK, PACK], F32, name="last_logit", tag="late_logits", align_bytes=64)
-        factor_of(3, behind_h[:, 1])
-        q_late = [q_third[:], behind_h[:, 1]]
-        late_logits = [behind_h[:, 0], last_logit[:]]
-        for n in range(2):
-            prob = sigmoid_of(2 + n, late_scores[n], q_late[n], late_logits[n])
-            nc.gpsimd.tensor_tensor(h[:, block(2 + n), :], prob[:], q_late[n], MULT)
-        early_scatter(0, first_dense)
-        early_scatter(1, early_caption_grad(1))
-        quantize(hq_r, E5M2, h, slice(half, LISTED))
-        early_scatter(2, early_caption_grad(2))
-        w_by_i = [
-            keep.tile([P, 2 * P, PACK], BF16, name="w_by_i", tag=tag, align_bytes=64) for tag in ("logit1", "late_logits")
-        ]
         w_words = w_by_d[:].rearrange("p i t -> p (i t)").bitcast(F32)
-        for u in range(2):
+
+        def turn_captions(u, tag):
+            by_i = keep.tile([P, 2 * P, PACK], BF16, name="w_by_i", tag=tag, align_bytes=64)
             turned = score_psum.tile([P, PACK, P], F32, name="w_turned", tag="score%d" % (u * (chunks - 1)))
             for j in range(PACK):
                 nc.tensor.transpose(turned[:, j, :], w_words[:, 2 * j + u : 2 * LISTED : 2 * PACK], ident_f32[:])
             nc.scalar.copy(
-                w_by_i[u][:].rearrange("m (e p) j -> m e p j", e=2),
+                by_i[:].rearrange("m (e p) j -> m e p j", e=2),
                 turned[:].rearrange("m j p -> m (j p)").bitcast(BF16).rearrange("m (j p e) -> m e p j", j=PACK, e=2),
             )
-        wq_i = [mx_operand("wq_i%d" % u, half, tag=tag) for u, tag in enumerate(("prob2", "prob1"))]
-        for u in range(2):
-            quantize(wq_i[u], E4M3, w_by_i[u], slice(0, half))
+            return by_i
+
+        third_prob = sigmoid_of(2, late_scores[0], q_third[:], behind_h[:, 0])
+        nc.gpsimd.tensor_tensor(h[:, block(2), :], third_prob[:], q_third[:], MULT)
+        factor_of(3, behind_h[:, 1])
+        wq_i = [mx_operand("wq_i0", half, tag="q_first")]
+        quantize(wq_i[0], E4M3, turn_captions(0, "logit1"), slice(0, half))
+        last_prob = sigmoid_of(3, late_scores[1], behind_h[:, 1], last_logit[:])
+        nc.gpsimd.tensor_tensor(h[:, block(3), :], last_prob[:], behind_h[:, 1], MULT)
+        early_scatter(0, first_dense)
+        early_scatter(1, early_caption_grad(1))
+        quantize(hq_r, E5M2, h, slice(half, LISTED))
+        early_scatter(2, early_caption_grad(2))
+        wq_i.append(mx_operand("wq_i1", half, tag="prob1"))
+        quantize(wq_i[1], E4M3, turn_captions(1, "late_logits"), slice(0, half))
         v_windows.append(keep.tile([P, TABLE], F32, name="v_window3", tag="late_logits", align_bytes=64))
         nc.gpsimd.memset(v_windows[V_WINDOWS][:], 0.0)
         for t in range(EARLY - 1):

@@ -134,8 +134,8 @@ def tile_attend_gmf_sig_vu_kernel(tc, uT, vT, y, us, ts, offs, uoffs, out_0, out
             quantize(xq_r, E4M3, x_by_r, cols)
         x_by_d = keep.tile([P, LISTED, PACK], BF16, name="x_by_d", align_bytes=64)
         nc.scalar.copy(
-            x_by_d[:].rearrange("p (j m) t -> p m j t", j=PACK),
-            x_planes[:].rearrange("p t (m j) -> p m j t", j=PACK),
+            x_by_d[:].rearrange("p (j m) t -> p m t j", j=PACK),
+            x_planes[:].rearrange("p t (m j) -> p m t j", j=PACK),
         )
         turn_images(last)
         v_planes = [keep.tile([P, TABLE], F32, name="v_plane", tag="plane%d" % t, align_bytes=64) for t in range(PACK)]

@@ -7,12 +7,10 @@ P = 128
 PACK = 4
 D = 512
 LISTED = 512
+HALF = LISTED // 2
 TABLE = 2048
 CHUNK = 128
-V_WINDOWS = 3
-U_WINDOWS = 2
-EARLY = 3
-PIECES = 2
+EARLY_WINDOWS = 5
 
 FLOPS = 3 * 2 * D * LISTED * LISTED
 BYTES = 4 * (4 * D * TABLE + LISTED * LISTED + LISTED + TABLE) + 2 * 2 * P * (LISTED // 16)
@@ -33,22 +31,23 @@ def tile_attend_gmf_sig_vu_kernel(tc, uT, vT, y, us, ts, offs, uoffs, out_0, out
     nc = tc.nc
     with ExitStack() as ctx:
         keep = ctx.enter_context(tc.tile_pool(name="keep", bufs=1))
-        staged = ctx.enter_context(tc.tile_pool(name="staged", bufs=6))
-        turn_psum = ctx.enter_context(tc.psum_pool(name="turn_psum", bufs=2))
-        score_psum = ctx.enter_context(tc.psum_pool(name="score_psum", bufs=1))
-        grad_psum = ctx.enter_context(tc.psum_pool(name="grad_psum", bufs=2))
+        psum = ctx.enter_context(tc.psum_pool(name="psum", bufs=1))
+
+        def held(name, shape, dtype, tag=""):
+            return keep.tile(shape, dtype, name=name, tag=tag or name, align_bytes=64)
+
+        def bank(name, shape, number, dtype=F32):
+            return psum.tile(shape, dtype, name=name, tag="bank%d" % number)
 
         def mx_operand(name, width=LISTED, tag=""):
-            codes = keep.tile([P, width], U32, name=name + "_codes", tag=tag, align_bytes=64)
-            scales = keep.tile([P, width], U8, name=name + "_scales", align_bytes=64)
-            return codes, scales
+            return held(name + "_codes", [P, width], U32, tag), held(name + "_scales", [P, width], U8)
 
-        def quantize(operand, fmt, source, cols):
+        def quantize(operand, fmt, cols, source):
             codes, scales = operand
             nc.vector.quantize_mx(
                 out=codes[:, cols].bitcast(fmt),
                 scales=scales[:, cols],
-                in_=source[:, cols, :].rearrange("p c t -> p (c t)"),
+                in_=source.rearrange("p c t -> p (c t)"),
             )
 
         def matmul(out, lhs, lhs_cols, rhs, rhs_fmt, rhs_cols):
@@ -65,19 +64,27 @@ def tile_attend_gmf_sig_vu_kernel(tc, uT, vT, y, us, ts, offs, uoffs, out_0, out
         def block(k):
             return slice(k * P, (k + 1) * P)
 
-        u_list = keep.tile([P, LISTED // 16], U16, name="u_list")
-        v_list = keep.tile([P, LISTED // 16], U16, name="v_list")
-        u_pair = keep.tile([P, 2, TABLE], F32, name="u_pair")
-        u_late = [keep.tile([P, TABLE], F32, name="u_late", tag="u_late%d" % n, align_bytes=64) for n in range(2)]
+        def half(n):
+            return slice(n * HALF, (n + 1) * HALF)
+
+        def entries(n):
+            return slice(n * HALF // 16, (n + 1) * HALF // 16)
+
+        last = PACK - 1
+        everything = slice(0, LISTED)
+
+        u_list = held("u_list", [P, LISTED // 16], U16)
+        v_list = held("v_list", [P, LISTED // 16], U16)
+        u_pair = held("u_pair", [P, 2, TABLE], F32)
+        u_late = [held("u_late%d" % n, [P, TABLE], F32) for n in range(2)]
         u_planes = [u_pair[:, 0, :], u_pair[:, 1, :], u_late[0][:], u_late[1][:]]
-        half = LISTED // 2
-        labels = [
-            keep.tile([P, PACK, half], F32, name="labels%d" % n, tag="labels%d" % n, align_bytes=64) for n in range(2)
-        ]
-        row_scale = keep.tile([P, PACK], F32, name="row_scale")
-        ts_window = keep.tile([P, TABLE], F32, name="ts_window")
+        v_planes = [held("v_plane%d" % t, [P, TABLE], F32) for t in range(PACK)]
+        labels = [held("labels%d" % n, [P, PACK, HALF], F32) for n in range(2)]
+        row_scale = held("row_scale", [P, PACK], F32)
+        ts_window = held("ts_window", [P, TABLE], F32)
         u_rows = uT.rearrange("(p t) c -> p t c", t=PACK)
         v_rows = vT.rearrange("(p t) c -> t p c", t=PACK)
+        y_rows = y.rearrange("b (p t) i -> p (b t) i", t=PACK)
 
         nc.scalar.dma_start(ts_window[P - 1 : P, :], ts[0:1, :])
         nc.scalar.dma_start(row_scale[:], us.rearrange("b (p t) o -> p (b t o)", t=PACK))
@@ -86,219 +93,217 @@ def tile_attend_gmf_sig_vu_kernel(tc, uT, vT, y, us, ts, offs, uoffs, out_0, out
         nc.sync.dma_start(u_list[:], uoffs)
         for n in range(2):
             nc.sync.dma_start(u_late[n][:], u_rows[:, 2 + n, :])
+        for t in range(PACK):
+            nc.sync.dma_start(v_planes[t][:], v_rows[t])
+        for n in range(2):
+            nc.sync.dma_start(labels[n][:], y_rows[:, :, half(n)])
 
-        warm = keep.tile([P, 8], F32, name="warm")
+        warm = held("warm", [P, 8], F32)
         nc.vector.memset(warm[:, 0:1], 0.0)
         nc.scalar.activation(warm[:, 1:2], warm[:, 0:1], SIGMOID)
         nc.vector.memset(ts_window[0 : P - 1, :], 0.0)
 
-        ident_f32 = keep.tile([P, P], F32, name="ident_f32")
+        ident_f32 = held("ident_f32", [P, P], F32)
         make_identity(nc, ident_f32[:])
+        ident_bf16 = held("ident_bf16", [P, P], BF16)
+        nc.scalar.copy(ident_bf16[:], ident_f32[:])
 
-        v_windows = [keep.tile([P, TABLE], F32, name="v_window%d" % k) for k in range(V_WINDOWS)]
-        u_windows = [keep.tile([P, TABLE], F32, name="u_window%d" % k) for k in range(U_WINDOWS)]
-        for window in v_windows + u_windows:
+        def cleared(k, tag=""):
+            window = held("window%d" % k, [P, TABLE], F32, tag)
             nc.gpsimd.memset(window[:], 0.0)
+            return window
 
-        ts_listed = keep.tile([P, LISTED], F32, name="ts_listed")
+        windows = [cleared(k) for k in range(EARLY_WINDOWS)]
+
+        ts_listed = held("ts_listed", [P, LISTED], F32)
         nc.vector.tensor_copy(ts_listed[:], ts_window[:].indirect(v_list[:]))
-        ts_turned = turn_psum.tile([P, PACK, P], F32, name="ts_turned", tag="turn")
+        ts_turned = bank("ts_turned", [P, PACK, P], 4)
         for k in range(PACK):
             nc.tensor.transpose(ts_turned[:, k, :], ts_listed[:, block(k)], ident_f32[:])
-        neg_ts = keep.tile([P, PACK], F32, name="neg_ts")
+        neg_ts = held("neg_ts", [P, PACK], F32)
         nc.scalar.activation(neg_ts[:], ts_turned[:, :, P - 1], COPY, scale=-1.0)
-        neg_ts_rows = grad_psum.tile([P, LISTED], F32, name="neg_ts_rows", tag="grad")
+        neg_ts_rows = bank("neg_ts_rows", [P, LISTED], 6)
         for k in range(PACK):
             nc.tensor.transpose(neg_ts_rows[:, block(k)], neg_ts[:, k : k + 1].to_broadcast([P, P]), ident_f32[:])
-
-        neg_scale = keep.tile([P, PACK, LISTED], F32, name="neg_scale")
+        neg_scale = held("neg_scale", [P, PACK, LISTED], F32)
         for t in range(PACK):
             nc.scalar.activation(neg_scale[:, t, :], neg_ts_rows[:], COPY, scale=row_scale[:, t : t + 1])
 
-        x_planes = keep.tile([P, PACK, LISTED], F32, name="x_planes", tag="x_planes")
-        x_by_r = keep.tile([P, D, PACK], BF16, name="x_by_r", align_bytes=64)
-        last = PACK - 1
-
-        def turn_images(t):
-            turned = turn_psum.tile([P, PACK, P], F32, name="x_turned", tag="turn")
+        def turn_plane(columns, ident, dtype, number, target):
+            turned = bank("turned", [P, PACK, P], number, dtype)
             for j in range(PACK):
-                nc.tensor.transpose(turned[:, j, :], x_planes[:, t, j:LISTED:PACK], ident_f32[:])
-            nc.scalar.copy(x_by_r[:, block(t), :], turned[:].rearrange("m j p -> m p j"))
+                nc.tensor.transpose(turned[:, j, :], columns(j), ident[:])
+            nc.scalar.copy(target, turned[:].rearrange("m j p -> m p j"))
 
+        x_planes = held("x_planes", [P, PACK, LISTED], F32)
+        x_by_r = held("x_by_r", [P, D, PACK], BF16)
+        x_by_d = held("x_by_d", [P, LISTED, PACK], BF16)
+        xq_r = mx_operand("xq_r")
+        xq_d = mx_operand("xq_d")
         for t in range(PACK):
             nc.vector.tensor_copy(x_planes[:, t, :], u_planes[t].indirect(u_list[:]))
-            if t < last:
-                turn_images(t)
-        xq_r = mx_operand("xq_r", last * P, tag="u_late1")
-        for cols in (slice(0, 2 * P), block(2)):
-            quantize(xq_r, E4M3, x_by_r, cols)
-        x_by_d = keep.tile([P, LISTED, PACK], BF16, name="x_by_d", align_bytes=64)
+            turn_plane(lambda j: x_planes[:, t, j:LISTED:PACK], ident_f32, F32, t, x_by_r[:, block(t), :])
         nc.scalar.copy(
             x_by_d[:].rearrange("p (j m) t -> p m t j", j=PACK),
             x_planes[:].rearrange("p t (m j) -> p m t j", j=PACK),
         )
-        turn_images(last)
-        v_planes = [keep.tile([P, TABLE], F32, name="v_plane", tag="plane%d" % t, align_bytes=64) for t in range(PACK)]
-        first_planes = (last - 1, 0, 1)
-        for t in first_planes:
-            nc.sync.dma_start(v_planes[t][:], v_rows[t])
-        pieces = [slice(k * TABLE // PIECES, (k + 1) * TABLE // PIECES) for k in range(PIECES)]
-        for cols in pieces:
-            nc.sync.dma_start(v_planes[last][:, cols], v_rows[last][:, cols])
-        y_rows = y.rearrange("b (p t) i -> p (b t) i", t=PACK)
         for n in range(2):
-            nc.sync.dma_start(labels[n][:], y_rows[:, :, n * half : (n + 1) * half])
+            quantize(xq_r, E4M3, half(n), x_by_r[:, half(n), :])
+        quantize(xq_d, E4M3, everything, x_by_d[:])
 
-        w_by_d = keep.tile([P, LISTED, PACK], BF16, name="w_by_d", align_bytes=64)
-        wq_d = mx_operand("wq_d", half)
-
-        for t in first_planes:
-            nc.vector.tensor_copy(w_by_d[:, :, t], v_planes[t][:].indirect(v_list[:]))
-            if t == 0:
-                xq_late = mx_operand("xq_late", LISTED + P, tag="plane0")
-                xq_d = [part[:, 0:LISTED] for part in xq_late]
-                xq_r_last = [part[:, LISTED:] for part in xq_late]
-                quantize(xq_d, E4M3, x_by_d, slice(0, LISTED))
-                quantize(xq_r_last, E4M3, x_by_r[:, block(last), :], block(0))
-        v_last_bf16 = keep.tile([P, TABLE], BF16, name="v_last_bf16", tag="plane%d" % (last - 1), align_bytes=64)
-        for cols in pieces:
-            nc.scalar.activation(v_last_bf16[:, cols], v_planes[last][:, cols], COPY)
-        nc.vector.tensor_copy(w_by_d[:, 0:half, last], v_planes[last][:].indirect(v_list[:, 0 : half // 16]))
-        nc.scalar.activation(w_by_d[:, half:, last], v_last_bf16[:].indirect(v_list[:, half // 16 :]), COPY)
+        w_planes = held("w_planes", [P, PACK, LISTED], F32)
+        w_by_d = held("w_by_d", [P, LISTED, PACK], BF16)
+        w_by_i = [held("w_by_i%d" % n, [P, HALF, PACK], BF16) for n in range(2)]
+        wq_d = [mx_operand("wq_d0", HALF)]
+        for t in range(last):
+            if t < 2:
+                nc.vector.tensor_copy(w_planes[:, t, :], v_planes[t][:].indirect(v_list[:]))
+            else:
+                nc.vector.tensor_copy(w_planes[:, t, half(0)], v_planes[t][:].indirect(v_list[:, entries(0)]))
+                nc.scalar.activation(w_planes[:, t, half(1)], v_planes[t][:].indirect(v_list[:, entries(1)]), COPY)
+            if t < 2:
+                turn_plane(lambda j: w_planes[:, t, j:LISTED:PACK], ident_f32, F32, 4 + t, w_by_i[0][:, block(t), :])
+        nc.vector.tensor_copy(
+            w_by_d[:, half(0), 0:last], w_planes[:, 0:last, half(0)].rearrange("p t i -> p i t")
+        )
+        nc.vector.tensor_copy(w_by_d[:, half(0), last], v_planes[last][:].indirect(v_list[:, entries(0)]))
+        nc.scalar.activation(w_planes[:, last, half(1)], v_planes[last][:].indirect(v_list[:, entries(1)]), COPY)
+        nc.scalar.copy(
+            w_by_d[:, half(1), :].rearrange("p (c i) t -> p c t i", i=4),
+            w_planes[:, :, half(1)].rearrange("p t (c i) -> p c t i", i=4),
+        )
         for c in range(2):
-            quantize(wq_d, E4M3, w_by_d, block(c))
+            quantize(wq_d[0], E4M3, block(c), w_by_d[:, block(c), :])
 
-        padded = mx_operand("hq_r", half + LISTED)
-        for part in padded:
-            nc.gpsimd.memset(part[:, 0:half], 0)
-        hq_r = [part[:, half:] for part in padded]
         chunks = LISTED // CHUNK
-        h = keep.tile([P, LISTED, PACK], BF16, name="h", align_bytes=64)
+        products = held("products", [P, 2, LISTED, PACK], F32, "u_pair")
+        q, logit = products[:, 0], products[:, 1]
+        prob = held("prob", [P, LISTED, PACK], F32, "u_late0")
+        h = held("h", [P, LISTED, PACK], BF16)
+        hq_r = mx_operand("hq_r")
+        scores = {}
 
-        def scores_of(c, captions):
-            score = score_psum.tile([P, PACK, CHUNK], F32, name="score", tag="score%d" % c)
+        def scores_of(c):
+            scores[c] = bank("score", [P, PACK, CHUNK], c)
             for t in range(PACK):
-                matmul(score[:, t, :], xq_d, block(t), captions, E4M3, block(c % 2))
-            return score
+                matmul(scores[c][:, t, :], xq_d, block(t), wq_d[c // 2], E4M3, block(c % 2))
 
-        def factor_of(c, q):
+        def factor_of(c):
             nc.vector.tensor_tensor(
-                q.rearrange("p (g i) t -> p g t i", i=2),
+                q[:, block(c), :].rearrange("p (g i) t -> p g t i", i=2),
                 labels[c // 2][:, :, block(c % 2)].rearrange("p t (g i) -> p g t i", i=2),
                 neg_scale[:, :, block(c)].rearrange("p t (g i) -> p g t i", i=2),
                 MULT,
             )
 
-        def sigmoid_of(c, score, q, logit):
-            nc.vector.tensor_tensor(logit, score[:].rearrange("p t i -> p i t"), q, MULT)
-            prob = keep.tile([P, CHUNK, PACK], F32, name="prob", tag="prob%d" % c, align_bytes=64)
-            nc.scalar.activation(prob[:], logit, SIGMOID)
-            return prob
+        def sigmoid_of(c):
+            nc.vector.tensor_tensor(
+                logit[:, block(c), :], scores[c][:].rearrange("p t i -> p i t"), q[:, block(c), :], MULT
+            )
+            nc.scalar.activation(prob[:, block(c), :], logit[:, block(c), :], SIGMOID)
 
-        scores = [scores_of(c, wq_d) for c in range(2)]
-        q_first = keep.tile([P, 2, CHUNK, PACK], F32, name="q_first", tag="q_first", align_bytes=64)
-        for c in range(2):
-            factor_of(c, q_first[:, c])
-        probs = []
-        for c in range(2):
-            logit = keep.tile([P, CHUNK, PACK], F32, name="logit", tag="logit%d" % c, align_bytes=64)
-            probs.append(sigmoid_of(c, scores[c], q_first[:, c], logit[:]))
-        wq_d_late = mx_operand("wq_d_late", half, tag="labels0")
-        quantize(wq_d_late, E4M3, w_by_d[:, half:, :], slice(0, half))
-        late_scores = [scores_of(c, wq_d_late) for c in range(2, chunks)]
-        q_third = keep.tile([P, CHUNK, PACK], F32, name="q_third")
-        factor_of(2, q_third[:])
-        for c in range(2):
-            nc.vector.tensor_tensor(h[:, block(c), :], probs[c][:], q_first[:, c], MULT)
-        for c in range(2):
-            quantize(hq_r, E5M2, h, block(c))
+        def h_of(c):
+            nc.vector.tensor_tensor(h[:, block(c), :], prob[:, block(c), :], q[:, block(c), :], MULT)
 
-        h_by_i = keep.tile([P, LISTED, PACK], BF16, name="h_by_i", tag="h_by_i", align_bytes=64)
-        hq_i = mx_operand("hq_i")
+        for c in range(2):
+            scores_of(c)
+        for c in range(2):
+            factor_of(c)
+        for c in range(2):
+            sigmoid_of(c)
+        wq_d.append(mx_operand("wq_d1", HALF, "labels0"))
+        quantize(wq_d[1], E4M3, half(0), w_by_d[:, half(1), :])
+        for c in range(2, chunks):
+            scores_of(c)
+        turn_plane(lambda j: w_planes[:, 2, j:LISTED:PACK], ident_f32, F32, 0, w_by_i[1][:, block(0), :])
+        turn_plane(lambda j: w_by_d[:, j:LISTED:PACK, last], ident_bf16, BF16, 1, w_by_i[1][:, block(1), :])
+        factor_of(2)
+        for c in range(2):
+            h_of(c)
+        for c in range(2):
+            quantize(hq_r, E5M2, block(c), h[:, block(c), :])
+        factor_of(3)
+        for c in range(2, chunks):
+            sigmoid_of(c)
+        for c in range(2, chunks):
+            h_of(c)
+        for c in range(2, chunks):
+            quantize(hq_r, E5M2, block(c), h[:, block(c), :])
+
         dv_rows = out_0.rearrange("(p t) c -> t p c", t=PACK)
         du_rows = out_1.rearrange("(p t) c -> t p c", t=PACK)
-        everything = slice(0, LISTED)
 
-        def early_caption_grad(t):
-            grad = grad_psum.tile([P, LISTED], F32, name="dv", tag="grad")
-            matmul(grad[:], xq_r, block(t), padded, E5M2, everything)
-            if t < EARLY - 1:
-                dense = staged.tile([P, half], F32, name="dense")
-            else:
-                dense = keep.tile([P, half], F32, name="late_dense", tag="prob%d" % (chunks - 1), align_bytes=64)
-            nc.scalar.copy(dense[:], grad[:, half:])
+        def grad(name, number, lhs, lhs_cols, rhs, cols):
+            sums = bank(name, [P, cols.stop - cols.start], number)
+            matmul(sums[:], lhs, lhs_cols, rhs, E5M2, cols)
+            return sums
+
+        def staged(name, source, copy, tag=""):
+            dense = held(name, [P, source.shape[1]], F32, tag)
+            copy(dense[:], source)
             return dense
 
-        def early_scatter(t, dense):
-            nc.vector.tensor_copy(v_windows[t][:].indirect(v_list[:, 0 : half // 16]), dense[:])
+        def first_half(window, places, dense):
+            nc.scalar.activation(window[:].indirect(places[:, entries(0)]), dense, COPY)
 
-        def caption_grad(t, first, pool, tag):
-            grad = pool.tile([P, LISTED], F32, name="dv", tag=tag)
-            if t < last:
-                matmul(grad[:], xq_r, block(t), hq_r, E5M2, everything)
-            else:
-                matmul(grad[:], xq_r_last, block(0), hq_r, E5M2, everything)
-            dense = staged.tile([P, LISTED - first], F32, name="dense")
-            nc.scalar.copy(dense[:], grad[:, first:])
-            window = v_windows[t]
-            nc.vector.tensor_copy(window[:].indirect(v_list[:, first // 16 :]), dense[:])
-            nc.sync.dma_start(dv_rows[t], window[:])
+        def second_half(window, places, dense, rows):
+            nc.vector.tensor_copy(window[:].indirect(places[:, entries(1)]), dense)
+            nc.sync.dma_start(rows, window[:])
 
-        def image_grad(t):
-            grad = grad_psum.tile([P, LISTED], F32, name="du", tag="grad")
-            matmul(grad[:], wq_i[t // 2], block(t % 2), hq_i, E5M2, everything)
-            dense = staged.tile([P, LISTED], F32, name="dense")
-            nc.scalar.copy(dense[:], grad[:])
-            window = u_windows[t % (U_WINDOWS + 1)]
-            nc.vector.tensor_copy(window[:].indirect(u_list[:]), dense[:])
-            nc.sync.dma_start(du_rows[t], window[:])
+        on_scalar, on_vector = nc.scalar.copy, nc.vector.tensor_copy
+        dv1a = grad("dv1a", 6, xq_r, block(1), hq_r, half(0))
+        dv0a = grad("dv0a", 3, xq_r, block(0), hq_r, half(0))
+        dv0b = grad("dv0b", 7, xq_r, block(0), hq_r, half(1))
+        dv1b = grad("dv1b", 0, xq_r, block(1), hq_r, half(1))
+        dv2 = grad("dv2", 1, xq_r, block(2), hq_r, everything)
+        wq_i = [mx_operand("wq_i0", HALF, "u_pair")]
+        first_half(windows[0], v_list, staged("d0a", dv0a[:], on_scalar)[:])
+        quantize(wq_i[0], E4M3, half(0), w_by_i[0][:])
+        d1a = staged("d1a", dv1a[:], on_vector, "u_late0")
+        d0b = staged("d0b", dv0b[:], on_vector)
+        first_half(windows[1], v_list, d1a[:])
+        second_half(windows[0], v_list, d0b[:], dv_rows[0])
+        d2 = staged("d2", dv2[:], on_scalar)
+        first_half(windows[2], v_list, d2[:, half(0)])
+        second_half(windows[1], v_list, staged("d1b", dv1b[:], on_vector)[:], dv_rows[1])
+        second_half(windows[2], v_list, d2[:, half(1)], dv_rows[2])
+        for k, tag in enumerate(("d0a", "d0b", "u_late0")):
+            windows.append(cleared(EARLY_WINDOWS + k, tag))
 
-        first_dense = early_caption_grad(0)
-        behind_h = keep.tile([P, 2, CHUNK, PACK], F32, name="behind_h", tag="prob1", align_bytes=64)
-        last_logit = keep.tile([P, CHUNK, PACK], F32, name="last_logit", tag="late_logits", align_bytes=64)
-        w_words = w_by_d[:].rearrange("p i t -> p (i t)").bitcast(F32)
-
-        def turn_captions(u, tag):
-            by_i = keep.tile([P, 2 * P, PACK], BF16, name="w_by_i", tag=tag, align_bytes=64)
-            turned = score_psum.tile([P, PACK, P], F32, name="w_turned", tag="score%d" % (u * (chunks - 1)))
-            for j in range(PACK):
-                nc.tensor.transpose(turned[:, j, :], w_words[:, 2 * j + u : 2 * LISTED : 2 * PACK], ident_f32[:])
-            nc.scalar.copy(
-                by_i[:].rearrange("m (e p) j -> m e p j", e=2),
-                turned[:].rearrange("m j p -> m (j p)").bitcast(BF16).rearrange("m (j p e) -> m e p j", j=PACK, e=2),
-            )
-            return by_i
-
-        third_prob = sigmoid_of(2, late_scores[0], q_third[:], behind_h[:, 0])
-        nc.gpsimd.tensor_tensor(h[:, block(2), :], third_prob[:], q_third[:], MULT)
-        factor_of(3, behind_h[:, 1])
-        wq_i = [mx_operand("wq_i0", half, tag="q_first")]
-        quantize(wq_i[0], E4M3, turn_captions(0, "logit1"), slice(0, half))
-        last_prob = sigmoid_of(3, late_scores[1], behind_h[:, 1], last_logit[:])
-        nc.gpsimd.tensor_tensor(h[:, block(3), :], last_prob[:], behind_h[:, 1], MULT)
-        early_scatter(0, first_dense)
-        early_scatter(1, early_caption_grad(1))
-        quantize(hq_r, E5M2, h, slice(half, LISTED))
-        early_scatter(2, early_caption_grad(2))
-        wq_i.append(mx_operand("wq_i1", half, tag="prob1"))
-        quantize(wq_i[1], E4M3, turn_captions(1, "late_logits"), slice(0, half))
-        v_windows.append(keep.tile([P, TABLE], F32, name="v_window3", tag="late_logits", align_bytes=64))
-        nc.gpsimd.memset(v_windows[V_WINDOWS][:], 0.0)
-        for t in range(EARLY - 1):
-            caption_grad(t, half, grad_psum, "grad")
-        caption_grad(EARLY - 1, half, turn_psum, "turn")
         h_words = h[:].rearrange("p i t -> p (i t)").bitcast(F32)
-        for u in range(2):
-            turned = grad_psum.tile([P, PACK, P], F32, name="h_turned", tag="grad")
+        h_turned = []
+        for u, number in enumerate((7, 1)):
+            turned = bank("h_turned", [P, PACK, P], number)
             for j in range(PACK):
                 nc.tensor.transpose(turned[:, j, :], h_words[:, 2 * j + u : 2 * LISTED : 2 * PACK], ident_f32[:])
-            nc.scalar.copy(
-                h_by_i[:].rearrange("m (p u e) j -> m u p e j", u=2, e=2)[:, u],
-                turned[:].rearrange("m j p -> m (j p)").bitcast(BF16).rearrange("m (j p e) -> m p e j", j=PACK, e=2),
+            h_turned.append(
+                turned[:].rearrange("m j p -> m (j p)").bitcast(BF16).rearrange("m (j p e) -> m p e j", j=PACK, e=2)
             )
-        quantize(hq_i, E5M2, h_by_i, everything)
-        u_windows.append(keep.tile([P, TABLE], F32, name="u_window2", tag="h_by_i", align_bytes=64))
-        nc.gpsimd.memset(u_windows[U_WINDOWS][:], 0.0)
-        caption_grad(last, 0, grad_psum, "grad")
-        for t in range(PACK):
-            image_grad(t)
+        dv3 = grad("dv3", 0, xq_r, block(last), hq_r, everything)
+        hq_i = mx_operand("hq_i")
+        h_by_i = [held("h_by_i%d" % n, [P, HALF, PACK], BF16) for n in range(2)]
+
+        def weave_h(n, copy):
+            for u in range(2):
+                copy(
+                    h_by_i[n][:].rearrange("m (p u e) j -> m u p e j", u=2, e=2)[:, u],
+                    h_turned[u][:, n * P // 2 : (n + 1) * P // 2],
+                )
+
+        weave_h(0, on_scalar)
+        first_half(windows[last], v_list, staged("d3a", dv3[:, half(0)], on_scalar)[:])
+        quantize(hq_i, E5M2, half(0), h_by_i[0][:])
+        weave_h(1, on_vector)
+        d3b = staged("d3b", dv3[:, half(1)], on_vector)
+        quantize(hq_i, E5M2, half(1), h_by_i[1][:])
+        second_half(windows[last], v_list, d3b[:], dv_rows[last])
+        wq_i.append(mx_operand("wq_i1", HALF, "d3b"))
+        quantize(wq_i[1], E4M3, half(0), w_by_i[1][:])
+
+        for t, numbers in enumerate(((6, 5), (3,), (2,), (4,))):
+            cuts = [half(0), half(1)] if t == 0 else [everything]
+            sums = [grad("du", number, wq_i[t // 2], block(t % 2), hq_i, cols) for number, cols in zip(numbers, cuts)]
+            parts = [sums[0][:, half(0)], sums[1][:] if t == 0 else sums[0][:, half(1)]]
+            window = windows[PACK + t]
+            first_half(window, u_list, staged("du%da" % t, parts[0], on_scalar)[:])
+            second_half(window, u_list, staged("du%db" % t, parts[1], on_vector)[:], du_rows[t])

from contextlib import ExitStack

import concourse.mybir as mybir
from concourse.masks import make_identity

P = 128
PACK = 4
D = 512
LISTED = 512
HALF = LISTED // 2
TABLE = 2048
CHUNK = 128
EARLY_WINDOWS = 5

FLOPS = 3 * 2 * D * LISTED * LISTED
BYTES = 4 * (4 * D * TABLE + LISTED * LISTED + LISTED + TABLE) + 2 * 2 * P * (LISTED // 16)

F32 = mybir.dt.float32
BF16 = mybir.dt.bfloat16
U32 = mybir.dt.uint32
U16 = mybir.dt.uint16
U8 = mybir.dt.uint8
E4M3 = mybir.dt.float8_e4m3fn_x4
E5M2 = mybir.dt.float8_e5m2_x4
MULT = mybir.AluOpType.mult
COPY = mybir.ActivationFunctionType.Copy
SIGMOID = mybir.ActivationFunctionType.Sigmoid


def tile_attend_gmf_sig_vu_kernel(tc, uT, vT, y, us, ts, offs, uoffs, out_0, out_1):
    nc = tc.nc
    with ExitStack() as ctx:
        keep = ctx.enter_context(tc.tile_pool(name="keep", bufs=1))
        psum = ctx.enter_context(tc.psum_pool(name="psum", bufs=1))

        def held(name, shape, dtype, tag=""):
            return keep.tile(shape, dtype, name=name, tag=tag or name, align_bytes=64)

        def bank(name, shape, number, dtype=F32):
            return psum.tile(shape, dtype, name=name, tag="bank%d" % number)

        def mx_operand(name, width=LISTED, tag=""):
            return held(name + "_codes", [P, width], U32, tag), held(name + "_scales", [P, width], U8)

        def quantize(operand, fmt, cols, source):
            codes, scales = operand
            nc.vector.quantize_mx(
                out=codes[:, cols].bitcast(fmt),
                scales=scales[:, cols],
                in_=source.rearrange("p c t -> p (c t)"),
            )

        def matmul(out, lhs, lhs_cols, rhs, rhs_fmt, rhs_cols):
            nc.tensor.matmul_mx(
                out=out,
                lhsT=lhs[0][:, lhs_cols].bitcast(E4M3),
                lhsT_scale=lhs[1][:, lhs_cols],
                rhs=rhs[0][:, rhs_cols].bitcast(rhs_fmt),
                rhs_scale=rhs[1][:, rhs_cols],
                start=True,
                stop=True,
            )

        def block(k):
            return slice(k * P, (k + 1) * P)

        def half(n):
            return slice(n * HALF, (n + 1) * HALF)

        def entries(n):
            return slice(n * HALF // 16, (n + 1) * HALF // 16)

        last = PACK - 1
        everything = slice(0, LISTED)

        u_list = held("u_list", [P, LISTED // 16], U16)
        v_list = held("v_list", [P, LISTED // 16], U16)
        u_pair = held("u_pair", [P, 2, TABLE], F32)
        u_late = [held("u_late%d" % n, [P, TABLE], F32) for n in range(2)]
        u_planes = [u_pair[:, 0, :], u_pair[:, 1, :], u_late[0][:], u_late[1][:]]
        v_planes = [held("v_plane%d" % t, [P, TABLE], F32) for t in range(PACK)]
        labels = [held("labels%d" % n, [P, PACK, HALF], F32) for n in range(2)]
        row_scale = held("row_scale", [P, PACK], F32)
        ts_window = held("ts_window", [P, TABLE], F32)
        u_rows = uT.rearrange("(p t) c -> p t c", t=PACK)
        v_rows = vT.rearrange("(p t) c -> t p c", t=PACK)
        y_rows = y.rearrange("b (p t) i -> p (b t) i", t=PACK)

        nc.scalar.dma_start(ts_window[P - 1 : P, :], ts[0:1, :])
        nc.scalar.dma_start(row_scale[:], us.rearrange("b (p t) o -> p (b t o)", t=PACK))
        nc.sync.dma_start(v_list[:], offs)
        nc.sync.dma_start(u_pair[:], u_rows[:, 0:2, :])
        nc.sync.dma_start(u_list[:], uoffs)
        for n in range(2):
            nc.sync.dma_start(u_late[n][:], u_rows[:, 2 + n, :])
        for t in range(PACK):
            nc.sync.dma_start(v_planes[t][:], v_rows[t])
        for n in range(2):
            nc.sync.dma_start(labels[n][:], y_rows[:, :, half(n)])

        warm = held("warm", [P, 8], F32)
        nc.vector.memset(warm[:, 0:1], 0.0)
        nc.scalar.activation(warm[:, 1:2], warm[:, 0:1], SIGMOID)
        nc.vector.memset(ts_window[0 : P - 1, :], 0.0)

        ident_f32 = held("ident_f32", [P, P], F32)
        make_identity(nc, ident_f32[:])
        ident_bf16 = held("ident_bf16", [P, P], BF16)
        nc.scalar.copy(ident_bf16[:], ident_f32[:])

        def cleared(k, tag=""):
            window = held("window%d" % k, [P, TABLE], F32, tag)
            nc.gpsimd.memset(window[:], 0.0)
            return window

        windows = [cleared(k) for k in range(EARLY_WINDOWS)]

        ts_listed = held("ts_listed", [P, LISTED], F32)
        nc.vector.tensor_copy(ts_listed[:], ts_window[:].indirect(v_list[:]))
        ts_turned = bank("ts_turned", [P, PACK, P], 4)
        for k in range(PACK):
            nc.tensor.transpose(ts_turned[:, k, :], ts_listed[:, block(k)], ident_f32[:])
        neg_ts = held("neg_ts", [P, PACK], F32)
        nc.scalar.activation(neg_ts[:], ts_turned[:, :, P - 1], COPY, scale=-1.0)
        neg_ts_rows = bank("neg_ts_rows", [P, LISTED], 6)
        for k in range(PACK):
            nc.tensor.transpose(neg_ts_rows[:, block(k)], neg_ts[:, k : k + 1].to_broadcast([P, P]), ident_f32[:])
        neg_scale = held("neg_scale", [P, PACK, LISTED], F32)
        for t in range(PACK):
            nc.scalar.activation(neg_scale[:, t, :], neg_ts_rows[:], COPY, scale=row_scale[:, t : t + 1])

        def turn_plane(columns, ident, dtype, number, target):
            turned = bank("turned", [P, PACK, P], number, dtype)
            for j in range(PACK):
                nc.tensor.transpose(turned[:, j, :], columns(j), ident[:])
            nc.scalar.copy(target, turned[:].rearrange("m j p -> m p j"))

        x_planes = held("x_planes", [P, PACK, LISTED], F32)
        x_by_r = held("x_by_r", [P, D, PACK], BF16)
        x_by_d = held("x_by_d", [P, LISTED, PACK], BF16)
        xq_r = mx_operand("xq_r")
        xq_d = mx_operand("xq_d")
        for t in range(PACK):
            nc.vector.tensor_copy(x_planes[:, t, :], u_planes[t].indirect(u_list[:]))
            turn_plane(lambda j: x_planes[:, t, j:LISTED:PACK], ident_f32, F32, t, x_by_r[:, block(t), :])
        nc.scalar.copy(
            x_by_d[:].rearrange("p (j m) t -> p m t j", j=PACK),
            x_planes[:].rearrange("p t (m j) -> p m t j", j=PACK),
        )
        for n in range(2):
            quantize(xq_r, E4M3, half(n), x_by_r[:, half(n), :])
        quantize(xq_d, E4M3, everything, x_by_d[:])

        w_planes = held("w_planes", [P, PACK, LISTED], F32)
        w_by_d = held("w_by_d", [P, LISTED, PACK], BF16)
        w_by_i = [held("w_by_i%d" % n, [P, HALF, PACK], BF16) for n in range(2)]
        wq_d = [mx_operand("wq_d0", HALF)]
        for t in range(last):
            if t < 2:
                nc.vector.tensor_copy(w_planes[:, t, :], v_planes[t][:].indirect(v_list[:]))
            else:
                nc.vector.tensor_copy(w_planes[:, t, half(0)], v_planes[t][:].indirect(v_list[:, entries(0)]))
                nc.scalar.activation(w_planes[:, t, half(1)], v_planes[t][:].indirect(v_list[:, entries(1)]), COPY)
            if t < 2:
                turn_plane(lambda j: w_planes[:, t, j:LISTED:PACK], ident_f32, F32, 4 + t, w_by_i[0][:, block(t), :])
        nc.vector.tensor_copy(
            w_by_d[:, half(0), 0:last], w_planes[:, 0:last, half(0)].rearrange("p t i -> p i t")
        )
        nc.vector.tensor_copy(w_by_d[:, half(0), last], v_planes[last][:].indirect(v_list[:, entries(0)]))
        nc.scalar.activation(w_planes[:, last, half(1)], v_planes[last][:].indirect(v_list[:, entries(1)]), COPY)
        nc.scalar.copy(
            w_by_d[:, half(1), :].rearrange("p (c i) t -> p c t i", i=4),
            w_planes[:, :, half(1)].rearrange("p t (c i) -> p c t i", i=4),
        )
        for c in range(2):
            quantize(wq_d[0], E4M3, block(c), w_by_d[:, block(c), :])

        chunks = LISTED // CHUNK
        products = held("products", [P, 2, LISTED, PACK], F32, "u_pair")
        q, logit = products[:, 0], products[:, 1]
        prob = held("prob", [P, LISTED, PACK], F32, "u_late0")
        h = held("h", [P, LISTED, PACK], BF16)
        hq_r = mx_operand("hq_r")
        scores = {}

        def scores_of(c):
            scores[c] = bank("score", [P, PACK, CHUNK], c)
            for t in range(PACK):
                matmul(scores[c][:, t, :], xq_d, block(t), wq_d[c // 2], E4M3, block(c % 2))

        def factor_of(c):
            nc.vector.tensor_tensor(
                q[:, block(c), :].rearrange("p (g i) t -> p g t i", i=2),
                labels[c // 2][:, :, block(c % 2)].rearrange("p t (g i) -> p g t i", i=2),
                neg_scale[:, :, block(c)].rearrange("p t (g i) -> p g t i", i=2),
                MULT,
            )

        def sigmoid_of(c):
            nc.vector.tensor_tensor(
                logit[:, block(c), :], scores[c][:].rearrange("p t i -> p i t"), q[:, block(c), :], MULT
            )
            nc.scalar.activation(prob[:, block(c), :], logit[:, block(c), :], SIGMOID)

        def h_of(c):
            nc.vector.tensor_tensor(h[:, block(c), :], prob[:, block(c), :], q[:, block(c), :], MULT)

        for c in range(2):
            scores_of(c)
        for c in range(2):
            factor_of(c)
        for c in range(2):
            sigmoid_of(c)
        wq_d.append(mx_operand("wq_d1", HALF, "labels0"))
        quantize(wq_d[1], E4M3, half(0), w_by_d[:, half(1), :])
        for c in range(2, chunks):
            scores_of(c)
        turn_plane(lambda j: w_planes[:, 2, j:LISTED:PACK], ident_f32, F32, 0, w_by_i[1][:, block(0), :])
        turn_plane(lambda j: w_by_d[:, j:LISTED:PACK, last], ident_bf16, BF16, 1, w_by_i[1][:, block(1), :])
        factor_of(2)
        for c in range(2):
            h_of(c)
        for c in range(2):
            quantize(hq_r, E5M2, block(c), h[:, block(c), :])
        factor_of(3)
        for c in range(2, chunks):
            sigmoid_of(c)
        for c in range(2, chunks):
            h_of(c)
        for c in range(2, chunks):
            quantize(hq_r, E5M2, block(c), h[:, block(c), :])

        dv_rows = out_0.rearrange("(p t) c -> t p c", t=PACK)
        du_rows = out_1.rearrange("(p t) c -> t p c", t=PACK)

        def grad(name, number, lhs, lhs_cols, rhs, cols):
            sums = bank(name, [P, cols.stop - cols.start], number)
            matmul(sums[:], lhs, lhs_cols, rhs, E5M2, cols)
            return sums

        def staged(name, source, copy, tag=""):
            dense = held(name, [P, source.shape[1]], F32, tag)
            copy(dense[:], source)
            return dense

        def first_half(window, places, dense):
            nc.scalar.activation(window[:].indirect(places[:, entries(0)]), dense, COPY)

        def second_half(window, places, dense, rows):
            nc.vector.tensor_copy(window[:].indirect(places[:, entries(1)]), dense)
            nc.sync.dma_start(rows, window[:])

        on_scalar, on_vector = nc.scalar.copy, nc.vector.tensor_copy
        dv1a = grad("dv1a", 6, xq_r, block(1), hq_r, half(0))
        dv0a = grad("dv0a", 3, xq_r, block(0), hq_r, half(0))
        dv0b = grad("dv0b", 7, xq_r, block(0), hq_r, half(1))
        dv1b = grad("dv1b", 0, xq_r, block(1), hq_r, half(1))
        dv2 = grad("dv2", 1, xq_r, block(2), hq_r, everything)
        wq_i = [mx_operand("wq_i0", HALF, "u_pair")]
        first_half(windows[0], v_list, staged("d0a", dv0a[:], on_scalar)[:])
        quantize(wq_i[0], E4M3, half(0), w_by_i[0][:])
        d1a = staged("d1a", dv1a[:], on_vector, "u_late0")
        d0b = staged("d0b", dv0b[:], on_vector)
        first_half(windows[1], v_list, d1a[:])
        second_half(windows[0], v_list, d0b[:], dv_rows[0])
        d2 = staged("d2", dv2[:], on_scalar)
        first_half(windows[2], v_list, d2[:, half(0)])
        second_half(windows[1], v_list, staged("d1b", dv1b[:], on_vector)[:], dv_rows[1])
        second_half(windows[2], v_list, d2[:, half(1)], dv_rows[2])
        for k, tag in enumerate(("d0a", "d0b", "u_late0")):
            windows.append(cleared(EARLY_WINDOWS + k, tag))

        h_words = h[:].rearrange("p i t -> p (i t)").bitcast(F32)
        h_turned = []
        for u, number in enumerate((7, 1)):
            turned = bank("h_turned", [P, PACK, P], number)
            for j in range(PACK):
                nc.tensor.transpose(turned[:, j, :], h_words[:, 2 * j + u : 2 * LISTED : 2 * PACK], ident_f32[:])
            h_turned.append(
                turned[:].rearrange("m j p -> m (j p)").bitcast(BF16).rearrange("m (j p e) -> m p e j", j=PACK, e=2)
            )
        dv3 = grad("dv3", 0, xq_r, block(last), hq_r, everything)
        hq_i = mx_operand("hq_i")
        h_by_i = [held("h_by_i%d" % n, [P, HALF, PACK], BF16) for n in range(2)]

        def weave_h(n, copy):
            for u in range(2):
                copy(
                    h_by_i[n][:].rearrange("m (p u e) j -> m u p e j", u=2, e=2)[:, u],
                    h_turned[u][:, n * P // 2 : (n + 1) * P // 2],
                )

        weave_h(0, on_scalar)
        first_half(windows[last], v_list, staged("d3a", dv3[:, half(0)], on_scalar)[:])
        quantize(hq_i, E5M2, half(0), h_by_i[0][:])
        weave_h(1, on_vector)
        d3b = staged("d3b", dv3[:, half(1)], on_vector)
        quantize(hq_i, E5M2, half(1), h_by_i[1][:])
        second_half(windows[last], v_list, d3b[:], dv_rows[last])
        wq_i.append(mx_operand("wq_i1", HALF, "d3b"))
        quantize(wq_i[1], E4M3, half(0), w_by_i[1][:])

        for t, numbers in enumerate(((6, 5), (3,), (2,), (4,))):
            cuts = [half(0), half(1)] if t == 0 else [everything]
            sums = [grad("du", number, wq_i[t // 2], block(t % 2), hq_i, cols) for number, cols in zip(numbers, cuts)]
            parts = [sums[0][:, half(0)], sums[1][:] if t == 0 else sums[0][:, half(1)]]
            window = windows[PACK + t]
            first_half(window, u_list, staged("du%da" % t, parts[0], on_scalar)[:])
            second_half(window, u_list, staged("du%db" % t, parts[1], on_vector)[:], du_rows[t])
